import numpy as np
import ml_dtypes


def mxq(x, axis, fmt="e4m3"):
    dtype, down = {"e4m3": (ml_dtypes.float8_e4m3fn, 7), "e5m2": (ml_dtypes.float8_e5m2, 14)}[fmt]
    v = np.moveaxis(np.asarray(x, np.float32).astype(ml_dtypes.bfloat16).astype(np.float64), axis, -1)
    blocks = v.reshape(v.shape[:-1] + (-1, 32))
    amax = np.abs(blocks).max(-1, keepdims=True)
    byte = np.maximum(np.where(amax > 0, np.frexp(amax)[1] - 1 + 127, 0) - down, 1)
    scale = np.exp2(byte - 127.0)
    codes = (blocks / scale).astype(np.float32).astype(dtype).astype(np.float64)
    return np.moveaxis((codes * scale).reshape(v.shape), -1, axis)


WIDE = False


def mx_kscale(k):
    if not WIDE:
        return np.ones(k)
    levels = np.array([10, -10, 5, -5, 0])
    if k % 512:
        return np.exp2(np.random.permutation(np.resize(levels, k // 32))).repeat(32)
    a = np.empty((k // 512, 16))
    for p in range(k // 512):
        a[p, :8] = np.random.permutation(np.resize(levels, 8))
        for g in range(8):
            far = levels[np.abs(levels - a[p, g]) >= 10]
            a[p, g + 8] = far[np.random.randint(len(far))]
    return np.exp2(a.ravel()).repeat(32)


def f64(x):
    return np.asarray(x).astype(np.float64)


def striped(idx):
    return np.tile(np.asarray(idx).reshape(-1, 16).T, (8, 1)).astype(np.uint16)


def unstriped(offs):
    return offs[:16].T.reshape(-1).astype(np.int64)


B, N, C, D, NQ = 1, 1024, 2048, 1024, 128


def eight(codes):
    return np.concatenate([codes[h].reshape(-1, 16).T for h in range(8)]).astype(np.uint16)


def uneight(offs):
    return np.stack([offs[16 * h:16 * h + 16].T.reshape(-1) for h in range(8)]).astype(np.int64)


def setup_inputs():
    n = np.random.standard_normal
    s = mx_kscale(D)[:, None]
    grid = lambda x: np.round(x * 32) / 32
    return {
        "qT": (n((B, D, NQ)) * s / np.sqrt(D)).astype(np.float32),
        "cb": (grid(n((D, C))) / s).astype(np.float32),
        "norm": np.tile(np.random.randint(32, 129, N) / 64.0, (128, 1)).astype(np.float32),
        "bias": np.tile(n(N), (128, 1)).astype(np.float32),
        "offs": eight(np.random.randint(0, C, (8, N))),
        "offs2": eight(np.random.randint(0, C, (8, N))),
    }


def reference(qT, cb, norm, bias, offs, offs2):
    k = []
    for part, offs_ in enumerate((offs, offs2,)):
        codes = uneight(offs_)
        k += [f64(cb)[512 * part + 64 * h:512 * part + 64 * h + 64][:, codes[h]] for h in range(8)]
    k = np.concatenate(k) * f64(norm)[:1]
    a = mxq(f64(qT), 1, "e4m3").transpose(0, 2, 1) @ mxq(k, 0, "e4m3")
    a = a + f64(bias)[:1]
    return a

@@ -1,0 +1,163 @@
+import concourse.mybir as mybir
+from concourse.masks import make_identity
+
+NQ, D, N, C = 128, 1024, 1024, 2048
+FLOPS = 2 * NQ * D * N
+
+F32 = mybir.dt.float32
+BF16 = mybir.dt.bfloat16
+U32 = mybir.dt.uint32
+U16 = mybir.dt.uint16
+U8 = mybir.dt.uint8
+FP8X4 = mybir.dt.float8_e4m3fn_x4
+MULT = mybir.AluOpType.mult
+ADD = mybir.AluOpType.add
+
+P = 128
+PACK = 4
+PASSES = D // (P * PACK)
+LIST = 16
+HALF = N // 2
+RUN = N // P
+
+PIECES = [(0, 512), (512, 256), (768, 256)]
+
+
+def tile_attend_pq_lin_bias_kernel(tc, qT, cb, norm, bias, offs, offs2, out):
+    nc = tc.nc
+    cb_planes = cb.rearrange("(g p t) c -> g t p c", g=PASSES, t=PACK)
+    q_rows = qT[0].rearrange("(g p t) q -> p g t q", g=PASSES, t=PACK)
+
+    with (
+        tc.tile_pool(name="keep", bufs=1) as keep,
+        tc.psum_pool(name="psum", bufs=1) as psum,
+    ):
+        lists = [keep.tile([P, N // LIST], U16, name=f"list{g}") for g in range(PASSES)]
+        norm_runs = keep.tile([P, RUN], F32, name="norm_runs")
+        identity = keep.tile([P, P], F32, name="identity")
+        norms = [keep.tile([P, HALF], F32, name=f"norm{a}", align_bytes=64) for a in range(2)]
+        bias_sb = keep.tile([P, N], F32, name="bias_sb")
+        planes = [
+            [keep.tile([P, C], F32, name=f"plane{g}{t}", align_bytes=64) for t in range(PACK)] for g in range(PASSES)
+        ]
+        q_raw = keep.tile([P, PASSES, PACK, NQ], F32, name="q_raw")
+        q_grouped = keep.tile([P, PASSES, NQ, PACK], BF16, name="q_grouped", align_bytes=64)
+        q_scales = keep.tile([P, PASSES * NQ], U8, name="q_scales", align_bytes=64)
+        k_raw = [[keep.tile([P, PACK, HALF], F32, name=f"k_raw{g}{h}") for h in range(2)] for g in range(PASSES)]
+        k_grouped = [keep.tile([P, N, PACK], BF16, name=f"k_grouped{g}", align_bytes=64) for g in range(PASSES)]
+        k_scales = [keep.tile([P, N], U8, name=f"k_scales{g}", align_bytes=64) for g in range(PASSES)]
+        out_sb = keep.tile([P, N], F32, name="out_sb")
+        banks = [psum.tile([P, width], F32, name=f"bank{i}") for i, (start, width) in enumerate(PIECES)]
+        spread = [psum.tile([P, PACK, P], F32, name=f"spread{e}") for e in range(RUN // PACK)]
+
+        nc.sync.dma_start(norm_runs[:], norm[0].rearrange("(p j) -> p j", j=RUN))
+        nc.sync.dma_start(planes[0][0][:], cb_planes[0, 0])
+        nc.sync.dma_start(lists[0][:], offs)
+        for t in range(1, PACK):
+            nc.sync.dma_start(planes[0][t][:], cb_planes[0, t])
+        nc.sync.dma_start(lists[1][:], offs2)
+        nc.sync.dma_start(planes[1][0][:], cb_planes[1, 0])
+        nc.sync.dma_start(planes[1][1][:], cb_planes[1, 1])
+        nc.sync.dma_start(q_raw[:], q_rows)
+        nc.sync.dma_start(planes[1][2][:], cb_planes[1, 2])
+        nc.sync.dma_start(planes[1][3][:], cb_planes[1, 3])
+        nc.sync.dma_start(bias_sb[:], bias)
+
+        make_identity(nc, identity[:])
+        for j in range(RUN):
+            column = norm_runs[:, j : j + 1]
+            nc.tensor.transpose(spread[j // PACK][:, j % PACK, :], column.to_broadcast([P, P]), identity[:])
+        for half in range(2):
+            runs = norms[half][:].rearrange("p (n e j) -> p e n j", e=RUN // PACK, j=PACK)
+            part = slice(half * P // 2, (half + 1) * P // 2)
+            for e, copy in ((0, nc.vector.tensor_copy), (1, nc.scalar.copy)):
+                copy(runs[:, e], spread[e][:, :, part].rearrange("p j n -> p n j"))
+
+        def gather(g, t, start, width):
+            entries = lists[g][:, start // LIST : (start + width) // LIST]
+            half, cols = start // HALF, slice(start % HALF, start % HALF + width)
+            nc.vector.tensor_tensor(
+                k_raw[g][half][:, t, cols], planes[g][t][:].indirect(entries), norms[half][:, cols], MULT
+            )
+
+        def interleave(g, half):
+            nc.scalar.copy(
+                k_grouped[g][:, half * HALF : (half + 1) * HALF, :].rearrange("p (c i) t -> p c t i", i=4),
+                k_raw[g][half][:].rearrange("p t (c i) -> p c t i", i=4),
+            )
+
+        def interleave_pair(copy, g, t, start, width):
+            half, cols = start // HALF, slice(start % HALF, start % HALF + width)
+            copy(
+                k_grouped[g][:, start : start + width, t : t + 2],
+                k_raw[g][half][:, t : t + 2, cols].rearrange("p t c -> p c t"),
+            )
+
+        def quantise(codes, g, start, width):
+            cols = slice(start, start + width)
+            nc.vector.quantize_mx(
+                out=codes[:, cols].bitcast(FP8X4),
+                scales=k_scales[g][:, cols],
+                in_=k_grouped[g][:, cols, :].rearrange("p c t -> p (c t)"),
+            )
+
+        def multiply(g, i):
+            start, width = PIECES[i]
+            cols = slice(start, start + width)
+            rows = slice(g * NQ, (g + 1) * NQ)
+            nc.tensor.matmul_mx(
+                out=banks[i][:],
+                lhsT=codes0[:, N + g * NQ : N + (g + 1) * NQ].bitcast(FP8X4),
+                lhsT_scale=q_scales[:, rows],
+                rhs=(codes0, codes1)[g][:, cols].bitcast(FP8X4),
+                rhs_scale=k_scales[g][:, cols],
+                start=(g == 0),
+                stop=(g == PASSES - 1),
+            )
+
+        def finish(i):
+            start, width = PIECES[i]
+            cols = slice(start, start + width)
+            nc.vector.tensor_tensor(out_sb[:, cols], banks[i][:], bias_sb[:, cols], ADD)
+            nc.sync.dma_start(out[0][:, cols], out_sb[:, cols])
+
+        for g, t in ((0, 0), (0, 1), (0, 2), (0, 3), (1, 0), (1, 1)):
+            for half in range(2):
+                gather(g, t, half * HALF, HALF)
+            for half in range(2):
+                if (g, t) == (0, 3):
+                    interleave(0, half)
+                if (g, t) == (1, 1):
+                    interleave_pair(nc.scalar.copy, 1, 0, half * HALF, HALF)
+        for half in range(PASSES):
+            nc.scalar.copy(q_grouped[:, half], q_raw[:, half].rearrange("p t q -> p q t"))
+
+        for half in range(2):
+            gather(1, 2, half * HALF, HALF)
+        gather(1, 3, *PIECES[0])
+        interleave_pair(nc.scalar.copy, 1, 2, *PIECES[0])
+        codes0 = keep.tile([P, N + PASSES * NQ], U32, name="codes0", tag="norm0", align_bytes=64)
+        quantise(codes0, 0, 0, N)
+        gather(1, 3, *PIECES[1])
+        interleave_pair(nc.scalar.copy, 1, 2, *PIECES[1])
+        nc.vector.quantize_mx(
+            out=codes0[:, N:].bitcast(FP8X4),
+            scales=q_scales[:],
+            in_=q_grouped[:].rearrange("p g q t -> p (g q t)"),
+        )
+        gather(1, 3, *PIECES[2])
+        interleave_pair(nc.scalar.copy, 1, 2, 768, 128)
+        interleave_pair(nc.vector.tensor_copy, 1, 2, 896, 128)
+
+        codes1 = keep.tile([P, N], U32, name="codes1", tag="plane13", align_bytes=64)
+        for i in range(len(PIECES)):
+            multiply(0, i)
+        quantise(codes1, 1, *PIECES[0])
+        multiply(1, 0)
+        quantise(codes1, 1, *PIECES[1])
+        multiply(1, 1)
+        finish(0)
+        quantise(codes1, 1, *PIECES[2])
+        multiply(1, 2)
+        finish(1)
+        finish(2)

@@ -18,6 +18,7 @@ PACK = 4
 PASSES = D // (P * PACK)
 LIST = 16
 HALF = N // 2
+QUARTER = N // 4
 RUN = N // P
 
 PIECES = [(0, 512), (512, 256), (768, 256)]
@@ -35,17 +36,19 @@ def tile_attend_pq_lin_bias_kernel(tc, qT, cb, norm, bias, offs, offs2, out):
         lists = [keep.tile([P, N // LIST], U16, name=f"list{g}") for g in range(PASSES)]
         norm_runs = keep.tile([P, RUN], F32, name="norm_runs")
         identity = keep.tile([P, P], F32, name="identity")
-        norms = [keep.tile([P, HALF], F32, name=f"norm{a}", align_bytes=64) for a in range(2)]
+        norm_sb = keep.tile([P, N], F32, name="norm_sb")
         bias_sb = keep.tile([P, N], F32, name="bias_sb")
         planes = [
             [keep.tile([P, C], F32, name=f"plane{g}{t}", align_bytes=64) for t in range(PACK)] for g in range(PASSES)
         ]
         q_raw = keep.tile([P, PASSES, PACK, NQ], F32, name="q_raw")
         q_grouped = keep.tile([P, PASSES, NQ, PACK], BF16, name="q_grouped", align_bytes=64)
+        q_codes = keep.tile([P, PASSES * NQ], U32, name="q_codes", align_bytes=64)
         q_scales = keep.tile([P, PASSES * NQ], U8, name="q_scales", align_bytes=64)
-        k_raw = [[keep.tile([P, PACK, HALF], F32, name=f"k_raw{g}{h}") for h in range(2)] for g in range(PASSES)]
+        k_raw = [keep.tile([P, PACK, N], F32, name=f"k_raw{g}") for g in range(PASSES)]
         k_grouped = [keep.tile([P, N, PACK], BF16, name=f"k_grouped{g}", align_bytes=64) for g in range(PASSES)]
         k_scales = [keep.tile([P, N], U8, name=f"k_scales{g}", align_bytes=64) for g in range(PASSES)]
+        early_codes = keep.tile([P, HALF], U32, name="early_codes", align_bytes=64)
         out_sb = keep.tile([P, N], F32, name="out_sb")
         banks = [psum.tile([P, width], F32, name=f"bank{i}") for i, (start, width) in enumerate(PIECES)]
         spread = [psum.tile([P, PACK, P], F32, name=f"spread{e}") for e in range(RUN // PACK)]
@@ -67,50 +70,49 @@ def tile_attend_pq_lin_bias_kernel(tc, qT, cb, norm, bias, offs, offs2, out):
         for j in range(RUN):
             column = norm_runs[:, j : j + 1]
             nc.tensor.transpose(spread[j // PACK][:, j % PACK, :], column.to_broadcast([P, P]), identity[:])
-        for half in range(2):
-            runs = norms[half][:].rearrange("p (n e j) -> p e n j", e=RUN // PACK, j=PACK)
-            part = slice(half * P // 2, (half + 1) * P // 2)
-            for e, copy in ((0, nc.vector.tensor_copy), (1, nc.scalar.copy)):
-                copy(runs[:, e], spread[e][:, :, part].rearrange("p j n -> p n j"))
+        runs = norm_sb[:].rearrange("p (n e j) -> p e n j", e=RUN // PACK, j=PACK)
+        for e, copy in ((0, nc.vector.tensor_copy), (1, nc.scalar.copy)):
+            copy(runs[:, e], spread[e][:].rearrange("p j n -> p n j"))
 
         def gather(g, t, start, width):
             entries = lists[g][:, start // LIST : (start + width) // LIST]
-            half, cols = start // HALF, slice(start % HALF, start % HALF + width)
-            nc.vector.tensor_tensor(
-                k_raw[g][half][:, t, cols], planes[g][t][:].indirect(entries), norms[half][:, cols], MULT
-            )
+            cols = slice(start, start + width)
+            nc.vector.tensor_tensor(k_raw[g][:, t, cols], planes[g][t][:].indirect(entries), norm_sb[:, cols], MULT)
 
-        def interleave(g, half):
+        def interleave(g, start, width):
+            cols = slice(start, start + width)
             nc.scalar.copy(
-                k_grouped[g][:, half * HALF : (half + 1) * HALF, :].rearrange("p (c i) t -> p c t i", i=4),
-                k_raw[g][half][:].rearrange("p t (c i) -> p c t i", i=4),
+                k_grouped[g][:, cols, :].rearrange("p (c i) t -> p c t i", i=4),
+                k_raw[g][:, :, cols].rearrange("p t (c i) -> p c t i", i=4),
             )
 
         def interleave_pair(copy, g, t, start, width):
-            half, cols = start // HALF, slice(start % HALF, start % HALF + width)
-            copy(
-                k_grouped[g][:, start : start + width, t : t + 2],
-                k_raw[g][half][:, t : t + 2, cols].rearrange("p t c -> p c t"),
-            )
+            cols = slice(start, start + width)
+            copy(k_grouped[g][:, cols, t : t + 2], k_raw[g][:, t : t + 2, cols].rearrange("p t c -> p c t"))
 
-        def quantise(codes, g, start, width):
+        def codes(g, start, width):
+            if g == 0 and start < HALF:
+                return early_codes[:, start : start + width].bitcast(FP8X4)
+            first = start - HALF if g == 0 else HALF + start
+            return late_codes[:, first : first + width].bitcast(FP8X4)
+
+        def quantise(g, start, width):
             cols = slice(start, start + width)
             nc.vector.quantize_mx(
-                out=codes[:, cols].bitcast(FP8X4),
+                out=codes(g, start, width),
                 scales=k_scales[g][:, cols],
                 in_=k_grouped[g][:, cols, :].rearrange("p c t -> p (c t)"),
             )
 
         def multiply(g, i):
             start, width = PIECES[i]
-            cols = slice(start, start + width)
             rows = slice(g * NQ, (g + 1) * NQ)
             nc.tensor.matmul_mx(
                 out=banks[i][:],
-                lhsT=codes0[:, N + g * NQ : N + (g + 1) * NQ].bitcast(FP8X4),
+                lhsT=q_codes[:, rows].bitcast(FP8X4),
                 lhsT_scale=q_scales[:, rows],
-                rhs=(codes0, codes1)[g][:, cols].bitcast(FP8X4),
-                rhs_scale=k_scales[g][:, cols],
+                rhs=codes(g, start, width),
+                rhs_scale=k_scales[g][:, start : start + width],
                 start=(g == 0),
                 stop=(g == PASSES - 1),
             )
@@ -121,43 +123,39 @@ def tile_attend_pq_lin_bias_kernel(tc, qT, cb, norm, bias, offs, offs2, out):
             nc.vector.tensor_tensor(out_sb[:, cols], banks[i][:], bias_sb[:, cols], ADD)
             nc.sync.dma_start(out[0][:, cols], out_sb[:, cols])
 
-        for g, t in ((0, 0), (0, 1), (0, 2), (0, 3), (1, 0), (1, 1)):
-            for half in range(2):
-                gather(g, t, half * HALF, HALF)
-            for half in range(2):
-                if (g, t) == (0, 3):
-                    interleave(0, half)
-                if (g, t) == (1, 1):
-                    interleave_pair(nc.scalar.copy, 1, 0, half * HALF, HALF)
-        for half in range(PASSES):
-            nc.scalar.copy(q_grouped[:, half], q_raw[:, half].rearrange("p t q -> p q t"))
-
-        for half in range(2):
-            gather(1, 2, half * HALF, HALF)
-        gather(1, 3, *PIECES[0])
-        interleave_pair(nc.scalar.copy, 1, 2, *PIECES[0])
-        codes0 = keep.tile([P, N + PASSES * NQ], U32, name="codes0", tag="norm0", align_bytes=64)
-        quantise(codes0, 0, 0, N)
-        gather(1, 3, *PIECES[1])
-        interleave_pair(nc.scalar.copy, 1, 2, *PIECES[1])
+        for t in range(PACK - 1):
+            gather(0, t, 0, N)
+        for start in (0, HALF):
+            gather(0, PACK - 1, start, HALF)
+            interleave(0, start, HALF)
+        quantise(0, 0, HALF)
+        for g in range(PASSES):
+            nc.scalar.copy(q_grouped[:, g], q_raw[:, g].rearrange("p t q -> p q t"))
         nc.vector.quantize_mx(
-            out=codes0[:, N:].bitcast(FP8X4),
+            out=q_codes[:].bitcast(FP8X4),
             scales=q_scales[:],
             in_=q_grouped[:].rearrange("p g q t -> p (g q t)"),
         )
-        gather(1, 3, *PIECES[2])
-        interleave_pair(nc.scalar.copy, 1, 2, 768, 128)
-        interleave_pair(nc.vector.tensor_copy, 1, 2, 896, 128)
+        gather(1, 0, 0, N)
+        for start in (0, HALF):
+            gather(1, 1, start, HALF)
+            interleave_pair(nc.scalar.copy, 1, 0, start, HALF)
+        gather(1, 2, 0, N)
+        for start, width in ((0, QUARTER), (QUARTER, QUARTER), (HALF, HALF)):
+            gather(1, 3, start, width)
+            for first in range(start, start + width, QUARTER):
+                interleave_pair(nc.scalar.copy, 1, 2, first, QUARTER)
 
-        codes1 = keep.tile([P, N], U32, name="codes1", tag="plane13", align_bytes=64)
+        late_codes = keep.tile([P, HALF + N], U32, name="late_codes", tag="plane13", align_bytes=64)
+        quantise(0, HALF, HALF)
         for i in range(len(PIECES)):
             multiply(0, i)
-        quantise(codes1, 1, *PIECES[0])
+        quantise(1, *PIECES[0])
         multiply(1, 0)
-        quantise(codes1, 1, *PIECES[1])
+        quantise(1, *PIECES[1])
         multiply(1, 1)
         finish(0)
-        quantise(codes1, 1, *PIECES[2])
+        quantise(1, *PIECES[2])
         multiply(1, 2)
         finish(1)
         finish(2)

@@ -19,7 +19,7 @@ PASSES = D // (P * PACK)
 LIST = 16
 HALF = N // 2
 QUARTER = N // 4
-RUN = N // P
+RUN = HALF // P
 
 PIECES = [(0, 512), (512, 256), (768, 256)]
 
@@ -34,26 +34,28 @@ def tile_attend_pq_lin_bias_kernel(tc, qT, cb, norm, bias, offs, offs2, out):
         tc.psum_pool(name="psum", bufs=1) as psum,
     ):
         lists = [keep.tile([P, N // LIST], U16, name=f"list{g}") for g in range(PASSES)]
-        norm_runs = keep.tile([P, RUN], F32, name="norm_runs")
+        norm_runs = keep.tile([P, 2, 2 * RUN], F32, name="norm_runs")
         identity = keep.tile([P, P], F32, name="identity")
         norm_sb = keep.tile([P, N], F32, name="norm_sb")
         bias_sb = keep.tile([P, N], F32, name="bias_sb")
         planes = [
             [keep.tile([P, C], F32, name=f"plane{g}{t}", align_bytes=64) for t in range(PACK)] for g in range(PASSES)
         ]
-        q_raw = keep.tile([P, PASSES, PACK, NQ], F32, name="q_raw")
+        q_raw = keep.tile([P, PASSES, PACK, NQ], F32, name="q_raw", align_bytes=64)
         q_grouped = keep.tile([P, PASSES, NQ, PACK], BF16, name="q_grouped", align_bytes=64)
-        q_codes = keep.tile([P, PASSES * NQ], U32, name="q_codes", align_bytes=64)
         q_scales = keep.tile([P, PASSES * NQ], U8, name="q_scales", align_bytes=64)
-        k_raw = [keep.tile([P, PACK, N], F32, name=f"k_raw{g}") for g in range(PASSES)]
-        k_grouped = [keep.tile([P, N, PACK], BF16, name=f"k_grouped{g}", align_bytes=64) for g in range(PASSES)]
+        k_raw = {(g, t): keep.tile([P, 2, N], F32, name=f"k_raw{g}{t}") for g in range(PASSES) for t in (0, 2)}
+        k_raw_first = keep.tile([P, 2, QUARTER], F32, name="k_raw_first", align_bytes=64)
+        q_codes = keep.tile([P, PASSES * NQ], U32, name="q_codes", align_bytes=64)
+        codes1 = keep.tile([P, N], U32, name="codes1", align_bytes=64)
+        k_grouped = [keep.tile([P, N, PACK], BF16, name="k_grouped0", align_bytes=64)]
         k_scales = [keep.tile([P, N], U8, name=f"k_scales{g}", align_bytes=64) for g in range(PASSES)]
         early_codes = keep.tile([P, HALF], U32, name="early_codes", align_bytes=64)
         out_sb = keep.tile([P, N], F32, name="out_sb")
         banks = [psum.tile([P, width], F32, name=f"bank{i}") for i, (start, width) in enumerate(PIECES)]
-        spread = [psum.tile([P, PACK, P], F32, name=f"spread{e}") for e in range(RUN // PACK)]
+        spread = [psum.tile([P, RUN, P], F32, name=f"spread{h}") for h in range(2)]
 
-        nc.sync.dma_start(norm_runs[:], norm[0].rearrange("(p j) -> p j", j=RUN))
+        nc.sync.dma_start(norm_runs[:, :, :RUN], norm[0].rearrange("(h p j) -> p h j", h=2, j=RUN))
         nc.sync.dma_start(planes[0][0][:], cb_planes[0, 0])
         nc.sync.dma_start(lists[0][:], offs)
         for t in range(1, PACK):
@@ -67,34 +69,33 @@ def tile_attend_pq_lin_bias_kernel(tc, qT, cb, norm, bias, offs, offs2, out):
         nc.sync.dma_start(bias_sb[:], bias)
 
         make_identity(nc, identity[:])
-        for j in range(RUN):
-            column = norm_runs[:, j : j + 1]
-            nc.tensor.transpose(spread[j // PACK][:, j % PACK, :], column.to_broadcast([P, P]), identity[:])
-        runs = norm_sb[:].rearrange("p (n e j) -> p e n j", e=RUN // PACK, j=PACK)
-        for e, copy in ((0, nc.vector.tensor_copy), (1, nc.scalar.copy)):
-            copy(runs[:, e], spread[e][:].rearrange("p j n -> p n j"))
+        for h, copy in ((0, nc.vector.tensor_copy), (1, nc.scalar.copy)):
+            for j in range(RUN):
+                column = norm_runs[:, h, j : j + 1]
+                nc.tensor.transpose(spread[h][:, j, :], column.to_broadcast([P, P]), identity[:])
+            runs = norm_sb[:, h * HALF : (h + 1) * HALF].rearrange("p (n j) -> p n j", j=RUN)
+            copy(runs, spread[h][:].rearrange("p j n -> p n j"))
+
+        def pair_rows(g, t, start, width):
+            tile = k_raw_first if (g, t // 2, start) == (1, 1, 0) else k_raw[g, t - t % 2]
+            return tile[:, :, start : start + width]
 
         def gather(g, t, start, width):
             entries = lists[g][:, start // LIST : (start + width) // LIST]
             cols = slice(start, start + width)
-            nc.vector.tensor_tensor(k_raw[g][:, t, cols], planes[g][t][:].indirect(entries), norm_sb[:, cols], MULT)
-
-        def interleave(g, start, width):
-            cols = slice(start, start + width)
-            nc.scalar.copy(
-                k_grouped[g][:, cols, :].rearrange("p (c i) t -> p c t i", i=4),
-                k_raw[g][:, :, cols].rearrange("p t (c i) -> p c t i", i=4),
-            )
+            row = pair_rows(g, t, start, width)[:, t % 2, :]
+            nc.vector.tensor_tensor(row, planes[g][t][:].indirect(entries), norm_sb[:, cols], MULT)
 
         def interleave_pair(copy, g, t, start, width):
             cols = slice(start, start + width)
-            copy(k_grouped[g][:, cols, t : t + 2], k_raw[g][:, t : t + 2, cols].rearrange("p t c -> p c t"))
+            copy(k_grouped[g][:, cols, t : t + 2], pair_rows(g, t, start, width).rearrange("p t c -> p c t"))
 
         def codes(g, start, width):
             if g == 0 and start < HALF:
                 return early_codes[:, start : start + width].bitcast(FP8X4)
-            first = start - HALF if g == 0 else HALF + start
-            return late_codes[:, first : first + width].bitcast(FP8X4)
+            if g == 0:
+                return late_codes[:, start - HALF : start - HALF + width].bitcast(FP8X4)
+            return codes1[:, start : start + width].bitcast(FP8X4)
 
         def quantise(g, start, width):
             cols = slice(start, start + width)
@@ -123,30 +124,35 @@ def tile_attend_pq_lin_bias_kernel(tc, qT, cb, norm, bias, offs, offs2, out):
             nc.vector.tensor_tensor(out_sb[:, cols], banks[i][:], bias_sb[:, cols], ADD)
             nc.sync.dma_start(out[0][:, cols], out_sb[:, cols])
 
-        for t in range(PACK - 1):
-            gather(0, t, 0, N)
         for start in (0, HALF):
-            gather(0, PACK - 1, start, HALF)
-            interleave(0, start, HALF)
-        quantise(0, 0, HALF)
+            gather(0, 0, start, HALF)
+        gather(0, 1, 0, N)
+        interleave_pair(nc.scalar.copy, 0, 0, 0, N)
+        gather(0, 2, 0, N)
+        gather(0, 3, 0, N)
+        for start in (0, HALF):
+            interleave_pair(nc.scalar.copy, 0, 2, start, HALF)
         for g in range(PASSES):
             nc.scalar.copy(q_grouped[:, g], q_raw[:, g].rearrange("p t q -> p q t"))
+        k_grouped.append(keep.tile([P, N, PACK], BF16, name="k_grouped1", tag="q_raw", align_bytes=64))
+        gather(1, 0, 0, N)
+        quantise(0, 0, HALF)
+        for start in (0, HALF):
+            gather(1, 1, start, HALF)
+            interleave_pair(nc.scalar.copy, 1, 0, start, HALF)
         nc.vector.quantize_mx(
             out=q_codes[:].bitcast(FP8X4),
             scales=q_scales[:],
             in_=q_grouped[:].rearrange("p g q t -> p (g q t)"),
         )
-        gather(1, 0, 0, N)
-        for start in (0, HALF):
-            gather(1, 1, start, HALF)
-            interleave_pair(nc.scalar.copy, 1, 0, start, HALF)
-        gather(1, 2, 0, N)
+        gather(1, 2, 0, QUARTER)
+        gather(1, 2, QUARTER, N - QUARTER)
         for start, width in ((0, QUARTER), (QUARTER, QUARTER), (HALF, HALF)):
             gather(1, 3, start, width)
             for first in range(start, start + width, QUARTER):
                 interleave_pair(nc.scalar.copy, 1, 2, first, QUARTER)
 
-        late_codes = keep.tile([P, HALF + N], U32, name="late_codes", tag="plane13", align_bytes=64)
+        late_codes = keep.tile([P, HALF], U32, name="late_codes", tag="k_raw_first", align_bytes=64)
         quantise(0, HALF, HALF)
         for i in range(len(PIECES)):
             multiply(0, i)

@@ -50,7 +50,6 @@ def tile_attend_pq_lin_bias_kernel(tc, qT, cb, norm, bias, offs, offs2, out):
         codes1 = keep.tile([P, N], U32, name="codes1", align_bytes=64)
         k_grouped = [keep.tile([P, N, PACK], BF16, name="k_grouped0", align_bytes=64)]
         k_scales = [keep.tile([P, N], U8, name=f"k_scales{g}", align_bytes=64) for g in range(PASSES)]
-        early_codes = keep.tile([P, HALF], U32, name="early_codes", align_bytes=64)
         out_sb = keep.tile([P, N], F32, name="out_sb")
         banks = [psum.tile([P, width], F32, name=f"bank{i}") for i, (start, width) in enumerate(PIECES)]
         spread = [psum.tile([P, RUN, P], F32, name=f"spread{h}") for h in range(2)]
@@ -91,11 +90,7 @@ def tile_attend_pq_lin_bias_kernel(tc, qT, cb, norm, bias, offs, offs2, out):
             copy(k_grouped[g][:, cols, t : t + 2], pair_rows(g, t, start, width).rearrange("p t c -> p c t"))
 
         def codes(g, start, width):
-            if g == 0 and start < HALF:
-                return early_codes[:, start : start + width].bitcast(FP8X4)
-            if g == 0:
-                return late_codes[:, start - HALF : start - HALF + width].bitcast(FP8X4)
-            return codes1[:, start : start + width].bitcast(FP8X4)
+            return (late_codes, codes1)[g][:, start : start + width].bitcast(FP8X4)
 
         def quantise(g, start, width):
             cols = slice(start, start + width)
@@ -129,14 +124,13 @@ def tile_attend_pq_lin_bias_kernel(tc, qT, cb, norm, bias, offs, offs2, out):
         gather(0, 1, 0, N)
         interleave_pair(nc.scalar.copy, 0, 0, 0, N)
         gather(0, 2, 0, N)
-        gather(0, 3, 0, N)
         for start in (0, HALF):
+            gather(0, 3, start, HALF)
             interleave_pair(nc.scalar.copy, 0, 2, start, HALF)
         for g in range(PASSES):
             nc.scalar.copy(q_grouped[:, g], q_raw[:, g].rearrange("p t q -> p q t"))
         k_grouped.append(keep.tile([P, N, PACK], BF16, name="k_grouped1", tag="q_raw", align_bytes=64))
         gather(1, 0, 0, N)
-        quantise(0, 0, HALF)
         for start in (0, HALF):
             gather(1, 1, start, HALF)
             interleave_pair(nc.scalar.copy, 1, 0, start, HALF)
@@ -152,12 +146,14 @@ def tile_attend_pq_lin_bias_kernel(tc, qT, cb, norm, bias, offs, offs2, out):
             for first in range(start, start + width, QUARTER):
                 interleave_pair(nc.scalar.copy, 1, 2, first, QUARTER)
 
-        late_codes = keep.tile([P, HALF], U32, name="late_codes", tag="k_raw_first", align_bytes=64)
-        quantise(0, HALF, HALF)
-        for i in range(len(PIECES)):
-            multiply(0, i)
+        late_codes = keep.tile([P, N], U32, name="late_codes", tag="k_raw_first", align_bytes=64)
+        quantise(0, 0, HALF)
+        multiply(0, 0)
         quantise(1, *PIECES[0])
         multiply(1, 0)
+        quantise(0, HALF, HALF)
+        multiply(0, 1)
+        multiply(0, 2)
         quantise(1, *PIECES[1])
         multiply(1, 1)
         finish(0)

@@ -27,7 +27,7 @@ PIECES = [(0, 512), (512, 256), (768, 256)]
 def tile_attend_pq_lin_bias_kernel(tc, qT, cb, norm, bias, offs, offs2, out):
     nc = tc.nc
     cb_planes = cb.rearrange("(g p t) c -> g t p c", g=PASSES, t=PACK)
-    q_rows = qT[0].rearrange("(g p t) q -> p g t q", g=PASSES, t=PACK)
+    q_rows = qT[0].rearrange("(g p t) q -> g p t q", g=PASSES, t=PACK)
 
     with (
         tc.tile_pool(name="keep", bufs=1) as keep,
@@ -41,7 +41,7 @@ def tile_attend_pq_lin_bias_kernel(tc, qT, cb, norm, bias, offs, offs2, out):
         planes = [
             [keep.tile([P, C], F32, name=f"plane{g}{t}", align_bytes=64) for t in range(PACK)] for g in range(PASSES)
         ]
-        q_raw = keep.tile([P, PASSES, PACK, NQ], F32, name="q_raw", align_bytes=64)
+        q_raw = [keep.tile([P, PACK, NQ], F32, name=f"q_raw{g}", align_bytes=64) for g in range(PASSES)]
         q_grouped = keep.tile([P, PASSES, NQ, PACK], BF16, name="q_grouped", align_bytes=64)
         q_scales = keep.tile([P, PASSES * NQ], U8, name="q_scales", align_bytes=64)
         k_raw = {(g, t): keep.tile([P, 2, N], F32, name=f"k_raw{g}{t}") for g in range(PASSES) for t in (0, 2)}
@@ -62,9 +62,10 @@ def tile_attend_pq_lin_bias_kernel(tc, qT, cb, norm, bias, offs, offs2, out):
         nc.sync.dma_start(lists[1][:], offs2)
         nc.sync.dma_start(planes[1][0][:], cb_planes[1, 0])
         nc.sync.dma_start(planes[1][1][:], cb_planes[1, 1])
-        nc.sync.dma_start(q_raw[:], q_rows)
+        nc.sync.dma_start(q_raw[0][:], q_rows[0])
         nc.sync.dma_start(planes[1][2][:], cb_planes[1, 2])
         nc.sync.dma_start(planes[1][3][:], cb_planes[1, 3])
+        nc.sync.dma_start(q_raw[1][:], q_rows[1])
         nc.sync.dma_start(bias_sb[:], bias)
 
         make_identity(nc, identity[:])
@@ -100,6 +101,17 @@ def tile_attend_pq_lin_bias_kernel(tc, qT, cb, norm, bias, offs, offs2, out):
                 in_=k_grouped[g][:, cols, :].rearrange("p c t -> p (c t)"),
             )
 
+        def round_q(g):
+            nc.scalar.copy(q_grouped[:, g], q_raw[g][:].rearrange("p t q -> p q t"))
+
+        def quantise_q(g):
+            rows = slice(g * NQ, (g + 1) * NQ)
+            nc.vector.quantize_mx(
+                out=q_codes[:, rows].bitcast(FP8X4),
+                scales=q_scales[:, rows],
+                in_=q_grouped[:, g].rearrange("p q t -> p (q t)"),
+            )
+
         def multiply(g, i):
             start, width = PIECES[i]
             rows = slice(g * NQ, (g + 1) * NQ)
@@ -113,10 +125,11 @@ def tile_attend_pq_lin_bias_kernel(tc, qT, cb, norm, bias, offs, offs2, out):
                 stop=(g == PASSES - 1),
             )
 
-        def finish(i):
-            start, width = PIECES[i]
-            cols = slice(start, start + width)
-            nc.vector.tensor_tensor(out_sb[:, cols], banks[i][:], bias_sb[:, cols], ADD)
+        def finish(start):
+            cols = slice(start, start + QUARTER)
+            i = max(i for i, piece in enumerate(PIECES) if piece[0] <= start)
+            bank = banks[i][:, start - PIECES[i][0] : start - PIECES[i][0] + QUARTER]
+            nc.vector.tensor_tensor(out_sb[:, cols], bank, bias_sb[:, cols], ADD)
             nc.sync.dma_start(out[0][:, cols], out_sb[:, cols])
 
         for start in (0, HALF):
@@ -127,22 +140,19 @@ def tile_attend_pq_lin_bias_kernel(tc, qT, cb, norm, bias, offs, offs2, out):
         for start in (0, HALF):
             gather(0, 3, start, HALF)
             interleave_pair(nc.scalar.copy, 0, 2, start, HALF)
-        for g in range(PASSES):
-            nc.scalar.copy(q_grouped[:, g], q_raw[:, g].rearrange("p t q -> p q t"))
-        k_grouped.append(keep.tile([P, N, PACK], BF16, name="k_grouped1", tag="q_raw", align_bytes=64))
+        round_q(0)
+        k_grouped.append(keep.tile([P, N, PACK], BF16, name="k_grouped1", tag="q_raw0", align_bytes=64))
         gather(1, 0, 0, N)
         for start in (0, HALF):
             gather(1, 1, start, HALF)
             interleave_pair(nc.scalar.copy, 1, 0, start, HALF)
-        nc.vector.quantize_mx(
-            out=q_codes[:].bitcast(FP8X4),
-            scales=q_scales[:],
-            in_=q_grouped[:].rearrange("p g q t -> p (g q t)"),
-        )
+        quantise_q(0)
         gather(1, 2, 0, QUARTER)
         gather(1, 2, QUARTER, N - QUARTER)
         for start, width in ((0, QUARTER), (QUARTER, QUARTER), (HALF, HALF)):
             gather(1, 3, start, width)
+            if start == HALF:
+                round_q(1)
             for first in range(start, start + width, QUARTER):
                 interleave_pair(nc.scalar.copy, 1, 2, first, QUARTER)
 
@@ -150,6 +160,7 @@ def tile_attend_pq_lin_bias_kernel(tc, qT, cb, norm, bias, offs, offs2, out):
         quantise(0, 0, HALF)
         multiply(0, 0)
         quantise(1, *PIECES[0])
+        quantise_q(1)
         multiply(1, 0)
         quantise(0, HALF, HALF)
         multiply(0, 1)
@@ -159,5 +170,5 @@ def tile_attend_pq_lin_bias_kernel(tc, qT, cb, norm, bias, offs, offs2, out):
         finish(0)
         quantise(1, *PIECES[2])
         multiply(1, 2)
-        finish(1)
-        finish(2)
+        for start in range(QUARTER, N, QUARTER):
+            finish(start)

@@ -12,6 +12,7 @@ U8 = mybir.dt.uint8
 FP8X4 = mybir.dt.float8_e4m3fn_x4
 MULT = mybir.AluOpType.mult
 ADD = mybir.AluOpType.add
+COPY = mybir.ActivationFunctionType.Copy
 
 P = 128
 PACK = 4
@@ -21,7 +22,8 @@ HALF = N // 2
 QUARTER = N // 4
 RUN = HALF // P
 
-PIECES = [(0, 512), (512, 256), (768, 256)]
+LOADS = [(0, 0), (0, 1), (0, 3), (0, 2), (1, 0), (1, 1), (1, 2), (1, 3)]
+SHARE = [HALF, HALF]
 
 
 def tile_attend_pq_lin_bias_kernel(tc, qT, cb, norm, bias, offs, offs2, out):
@@ -36,139 +38,135 @@ def tile_attend_pq_lin_bias_kernel(tc, qT, cb, norm, bias, offs, offs2, out):
         lists = [keep.tile([P, N // LIST], U16, name=f"list{g}") for g in range(PASSES)]
         norm_runs = keep.tile([P, 2, 2 * RUN], F32, name="norm_runs")
         identity = keep.tile([P, P], F32, name="identity")
-        norm_sb = keep.tile([P, N], F32, name="norm_sb")
+        norm_sb = keep.tile([P, HALF], F32, name="norm_sb")
         bias_sb = keep.tile([P, N], F32, name="bias_sb")
         planes = [
             [keep.tile([P, C], F32, name=f"plane{g}{t}", align_bytes=64) for t in range(PACK)] for g in range(PASSES)
         ]
         q_raw = [keep.tile([P, PACK, NQ], F32, name=f"q_raw{g}", align_bytes=64) for g in range(PASSES)]
-        q_grouped = keep.tile([P, PASSES, NQ, PACK], BF16, name="q_grouped", align_bytes=64)
-        q_scales = keep.tile([P, PASSES * NQ], U8, name="q_scales", align_bytes=64)
-        k_raw = {(g, t): keep.tile([P, 2, N], F32, name=f"k_raw{g}{t}") for g in range(PASSES) for t in (0, 2)}
-        k_raw_first = keep.tile([P, 2, QUARTER], F32, name="k_raw_first", align_bytes=64)
-        q_codes = keep.tile([P, PASSES * NQ], U32, name="q_codes", align_bytes=64)
-        codes1 = keep.tile([P, N], U32, name="codes1", align_bytes=64)
-        k_grouped = [keep.tile([P, N, PACK], BF16, name="k_grouped0", align_bytes=64)]
-        k_scales = [keep.tile([P, N], U8, name=f"k_scales{g}", align_bytes=64) for g in range(PASSES)]
+        q_codes = [keep.tile([P, NQ], U32, name=f"q_codes{g}", align_bytes=64) for g in range(PASSES)]
+        q_scales = [keep.tile([P, NQ], U8, name=f"q_scales{g}", align_bytes=64) for g in range(PASSES)]
+        halves = [(g, h) for g in range(PASSES) for h in range(2)]
+        k_grouped = [keep.tile([P, N, PACK], BF16, name=f"k_grouped{g}", align_bytes=64) for g in range(PASSES)]
+        k_codes = {gh: keep.tile([P, HALF], U32, name="k_codes%d%d" % gh, align_bytes=64) for gh in halves}
+        k_scales = {gh: keep.tile([P, HALF], U8, name="k_scales%d%d" % gh, align_bytes=64) for gh in halves}
         out_sb = keep.tile([P, N], F32, name="out_sb")
-        banks = [psum.tile([P, width], F32, name=f"bank{i}") for i, (start, width) in enumerate(PIECES)]
+        banks = [psum.tile([P, QUARTER], F32, name=f"bank{i}") for i in range(4)]
         spread = [psum.tile([P, RUN, P], F32, name=f"spread{h}") for h in range(2)]
 
         nc.sync.dma_start(norm_runs[:, :, :RUN], norm[0].rearrange("(h p j) -> p h j", h=2, j=RUN))
-        nc.sync.dma_start(planes[0][0][:], cb_planes[0, 0])
-        nc.sync.dma_start(lists[0][:], offs)
-        for t in range(1, PACK):
-            nc.sync.dma_start(planes[0][t][:], cb_planes[0, t])
-        nc.sync.dma_start(lists[1][:], offs2)
-        nc.sync.dma_start(planes[1][0][:], cb_planes[1, 0])
-        nc.sync.dma_start(planes[1][1][:], cb_planes[1, 1])
-        nc.sync.dma_start(q_raw[0][:], q_rows[0])
-        nc.sync.dma_start(planes[1][2][:], cb_planes[1, 2])
-        nc.sync.dma_start(planes[1][3][:], cb_planes[1, 3])
-        nc.sync.dma_start(q_raw[1][:], q_rows[1])
+        for row, (g, t) in enumerate(LOADS):
+            if row == PACK:
+                nc.sync.dma_start(lists[1][:], offs2)
+            nc.sync.dma_start(planes[g][t][:], cb_planes[g, t])
+            if row == 0:
+                nc.sync.dma_start(lists[0][:], offs)
+        for g in range(PASSES):
+            nc.sync.dma_start(q_raw[g][:], q_rows[g])
         nc.sync.dma_start(bias_sb[:], bias)
 
         make_identity(nc, identity[:])
-        for h, copy in ((0, nc.vector.tensor_copy), (1, nc.scalar.copy)):
+        for h in range(2):
             for j in range(RUN):
                 column = norm_runs[:, h, j : j + 1]
                 nc.tensor.transpose(spread[h][:, j, :], column.to_broadcast([P, P]), identity[:])
-            runs = norm_sb[:, h * HALF : (h + 1) * HALF].rearrange("p (n j) -> p n j", j=RUN)
-            copy(runs, spread[h][:].rearrange("p j n -> p n j"))
+        nc.scalar.copy(norm_sb[:].rearrange("p (n j) -> p n j", j=RUN), spread[0][:].rearrange("p j n -> p n j"))
 
-        def pair_rows(g, t, start, width):
-            tile = k_raw_first if (g, t // 2, start) == (1, 1, 0) else k_raw[g, t - t % 2]
-            return tile[:, :, start : start + width]
+        ring = keep.tile([P, 3, N], F32, name="ring", tag="norm_runs")
 
-        def gather(g, t, start, width):
-            entries = lists[g][:, start // LIST : (start + width) // LIST]
-            cols = slice(start, start + width)
-            row = pair_rows(g, t, start, width)[:, t % 2, :]
-            nc.vector.tensor_tensor(row, planes[g][t][:].indirect(entries), norm_sb[:, cols], MULT)
+        def entries(row, start, width):
+            return lists[LOADS[row][0]][:, start // LIST : (start + width) // LIST]
 
-        def interleave_pair(copy, g, t, start, width):
-            cols = slice(start, start + width)
-            copy(k_grouped[g][:, cols, t : t + 2], pair_rows(g, t, start, width).rearrange("p t c -> p c t"))
+        def gather(row):
+            g, t = LOADS[row]
+            first = row % 2 * HALF
+            for start in range(0, first, QUARTER):
+                window = planes[g][t][:].bitcast(U32).indirect(entries(row, start, QUARTER))
+                nc.vector.tensor_copy(ring[:, row % 3, start : start + QUARTER].bitcast(U32), window)
+            nc.scalar.activation(ring[:, row % 3, first:], planes[g][t][:].indirect(entries(row, first, N - first)), COPY)
 
-        def codes(g, start, width):
-            return (late_codes, codes1)[g][:, start : start + width].bitcast(FP8X4)
+        def weave(pair):
+            g, t = pair // 2, pair % 2 * 2
+            first, second = sorted((2 * pair % 3, (2 * pair + 1) % 3))
+            rows = ring[:, first : second + 1 : second - first, :]
+            for start, end in ((0, QUARTER), (QUARTER, SHARE[g])):
+                nc.gpsimd.tensor_tensor(
+                    k_grouped[g][:, start:end, t : t + 2],
+                    rows[:, :, start:end].rearrange("p t c -> p c t"),
+                    norm_sb[:, start:end].unsqueeze(2).to_broadcast([P, end - start, 2]),
+                    MULT,
+                )
+            for h, start, end in ((0, SHARE[g], HALF), (1, HALF, N)):
+                if start < end:
+                    runs = spread[h][:, :, start % HALF // RUN :].rearrange("p j n -> p n j")
+                    nc.vector.tensor_tensor(
+                        k_grouped[g][:, start:end, t : t + 2].rearrange("p (n j) t -> p n j t", j=RUN),
+                        rows[:, :, start:end].rearrange("p t (n j) -> p n j t", j=RUN),
+                        runs.unsqueeze(3).to_broadcast([P, (end - start) // RUN, RUN, 2]),
+                        MULT,
+                    )
 
-        def quantise(g, start, width):
+        def quantise(g, h, start, width):
             cols = slice(start, start + width)
             nc.vector.quantize_mx(
-                out=codes(g, start, width),
-                scales=k_scales[g][:, cols],
-                in_=k_grouped[g][:, cols, :].rearrange("p c t -> p (c t)"),
+                out=k_codes[g, h][:, cols].bitcast(FP8X4),
+                scales=k_scales[g, h][:, cols],
+                in_=k_grouped[g][:, h * HALF + start : h * HALF + start + width, :].rearrange("p c t -> p (c t)"),
             )
 
         def round_q(g):
-            nc.scalar.copy(q_grouped[:, g], q_raw[g][:].rearrange("p t q -> p q t"))
+            nc.scalar.copy(q_grouped[g], q_raw[g][:].rearrange("p t q -> p q t"))
 
         def quantise_q(g):
-            rows = slice(g * NQ, (g + 1) * NQ)
             nc.vector.quantize_mx(
-                out=q_codes[:, rows].bitcast(FP8X4),
-                scales=q_scales[:, rows],
-                in_=q_grouped[:, g].rearrange("p q t -> p (q t)"),
+                out=q_codes[g][:].bitcast(FP8X4),
+                scales=q_scales[g][:],
+                in_=q_grouped[g].rearrange("p q t -> p (q t)"),
             )
 
         def multiply(g, i):
-            start, width = PIECES[i]
-            rows = slice(g * NQ, (g + 1) * NQ)
+            h, first = divmod(i * QUARTER, HALF)
+            cols = slice(first, first + QUARTER)
             nc.tensor.matmul_mx(
                 out=banks[i][:],
-                lhsT=q_codes[:, rows].bitcast(FP8X4),
-                lhsT_scale=q_scales[:, rows],
-                rhs=codes(g, start, width),
-                rhs_scale=k_scales[g][:, start : start + width],
+                lhsT=q_codes[g][:].bitcast(FP8X4),
+                lhsT_scale=q_scales[g][:],
+                rhs=k_codes[g, h][:, cols].bitcast(FP8X4),
+                rhs_scale=k_scales[g, h][:, cols],
                 start=(g == 0),
                 stop=(g == PASSES - 1),
             )
 
-        def finish(start):
-            cols = slice(start, start + QUARTER)
-            i = max(i for i, piece in enumerate(PIECES) if piece[0] <= start)
-            bank = banks[i][:, start - PIECES[i][0] : start - PIECES[i][0] + QUARTER]
-            nc.vector.tensor_tensor(out_sb[:, cols], bank, bias_sb[:, cols], ADD)
+        def finish(i):
+            cols = slice(i * QUARTER, (i + 1) * QUARTER)
+            nc.vector.tensor_tensor(out_sb[:, cols], banks[i][:], bias_sb[:, cols], ADD)
             nc.sync.dma_start(out[0][:, cols], out_sb[:, cols])
 
-        for start in (0, HALF):
-            gather(0, 0, start, HALF)
-        gather(0, 1, 0, N)
-        interleave_pair(nc.scalar.copy, 0, 0, 0, N)
-        gather(0, 2, 0, N)
-        for start in (0, HALF):
-            gather(0, 3, start, HALF)
-            interleave_pair(nc.scalar.copy, 0, 2, start, HALF)
-        round_q(0)
-        k_grouped.append(keep.tile([P, N, PACK], BF16, name="k_grouped1", tag="q_raw0", align_bytes=64))
-        gather(1, 0, 0, N)
-        for start in (0, HALF):
-            gather(1, 1, start, HALF)
-            interleave_pair(nc.scalar.copy, 1, 0, start, HALF)
-        quantise_q(0)
-        gather(1, 2, 0, QUARTER)
-        gather(1, 2, QUARTER, N - QUARTER)
-        for start, width in ((0, QUARTER), (QUARTER, QUARTER), (HALF, HALF)):
-            gather(1, 3, start, width)
-            if start == HALF:
-                round_q(1)
-            for first in range(start, start + width, QUARTER):
-                interleave_pair(nc.scalar.copy, 1, 2, first, QUARTER)
+        for pair in range(2 * PASSES):
+            gather(2 * pair)
+            gather(2 * pair + 1)
+            weave(pair)
+            if pair == 1:
+                quantise(0, 1, 0, HALF)
+                quantise(0, 0, 0, HALF)
 
-        late_codes = keep.tile([P, N], U32, name="late_codes", tag="k_raw_first", align_bytes=64)
-        quantise(0, 0, HALF)
-        multiply(0, 0)
-        quantise(1, *PIECES[0])
+        q_both = keep.tile([P, PASSES, NQ, PACK], BF16, name="q_both", tag="plane13", align_bytes=64)
+        q_grouped = [q_both[:, g] for g in range(PASSES)]
+        round_q(0)
+        round_q(1)
+        quantise_q(0)
         quantise_q(1)
-        multiply(1, 0)
-        quantise(0, HALF, HALF)
-        multiply(0, 1)
-        multiply(0, 2)
-        quantise(1, *PIECES[1])
-        multiply(1, 1)
-        finish(0)
-        quantise(1, *PIECES[2])
+        quantise(1, 1, 0, HALF)
+        for i in (2, 3):
+            multiply(0, i)
         multiply(1, 2)
-        for start in range(QUARTER, N, QUARTER):
-            finish(start)
+        multiply(1, 3)
+        quantise(1, 0, 0, QUARTER)
+        multiply(0, 0)
+        multiply(1, 0)
+        finish(2)
+        quantise(1, 0, QUARTER, QUARTER)
+        multiply(0, 1)
+        multiply(1, 1)
+        for i in (3, 0, 1):
+            finish(i)

@@ -23,7 +23,7 @@ QUARTER = N // 4
 RUN = HALF // P
 
 LOADS = [(0, 0), (0, 1), (0, 3), (0, 2), (1, 0), (1, 1), (1, 2), (1, 3)]
-SHARE = [HALF, HALF]
+SHARE = [HALF, HALF, HALF]
 
 
 def tile_attend_pq_lin_bias_kernel(tc, qT, cb, norm, bias, offs, offs2, out):
@@ -77,34 +77,40 @@ def tile_attend_pq_lin_bias_kernel(tc, qT, cb, norm, bias, offs, offs2, out):
         def entries(row, start, width):
             return lists[LOADS[row][0]][:, start // LIST : (start + width) // LIST]
 
+        def slot(row):
+            return 1 if row % 2 else row % 4
+
         def gather(row):
             g, t = LOADS[row]
             first = row % 2 * HALF
             for start in range(0, first, QUARTER):
                 window = planes[g][t][:].bitcast(U32).indirect(entries(row, start, QUARTER))
-                nc.vector.tensor_copy(ring[:, row % 3, start : start + QUARTER].bitcast(U32), window)
-            nc.scalar.activation(ring[:, row % 3, first:], planes[g][t][:].indirect(entries(row, first, N - first)), COPY)
+                nc.vector.tensor_copy(ring[:, slot(row), start : start + QUARTER].bitcast(U32), window)
+            nc.scalar.activation(ring[:, slot(row), first:], planes[g][t][:].indirect(entries(row, first, N - first)), COPY)
 
-        def weave(pair):
+        def pair_rows(pair):
+            if pair == 3:
+                return ring[:, 2:0:-1, :]
+            return ring[:, pair % 2 : pair % 2 + 2, :]
+
+        def weave_on_gpsimd(pair, start, end):
             g, t = pair // 2, pair % 2 * 2
-            first, second = sorted((2 * pair % 3, (2 * pair + 1) % 3))
-            rows = ring[:, first : second + 1 : second - first, :]
-            for start, end in ((0, QUARTER), (QUARTER, SHARE[g])):
-                nc.gpsimd.tensor_tensor(
-                    k_grouped[g][:, start:end, t : t + 2],
-                    rows[:, :, start:end].rearrange("p t c -> p c t"),
-                    norm_sb[:, start:end].unsqueeze(2).to_broadcast([P, end - start, 2]),
-                    MULT,
-                )
-            for h, start, end in ((0, SHARE[g], HALF), (1, HALF, N)):
-                if start < end:
-                    runs = spread[h][:, :, start % HALF // RUN :].rearrange("p j n -> p n j")
-                    nc.vector.tensor_tensor(
-                        k_grouped[g][:, start:end, t : t + 2].rearrange("p (n j) t -> p n j t", j=RUN),
-                        rows[:, :, start:end].rearrange("p t (n j) -> p n j t", j=RUN),
-                        runs.unsqueeze(3).to_broadcast([P, (end - start) // RUN, RUN, 2]),
-                        MULT,
-                    )
+            nc.gpsimd.tensor_tensor(
+                k_grouped[g][:, start:end, t : t + 2],
+                pair_rows(pair)[:, :, start:end].rearrange("p t c -> p c t"),
+                norm_sb[:, start:end].unsqueeze(2).to_broadcast([P, end - start, 2]),
+                MULT,
+            )
+
+        def weave_on_vector(pair, start, end):
+            g, t = pair // 2, pair % 2 * 2
+            runs = spread[start // HALF][:, :, start % HALF // RUN :].rearrange("p j n -> p n j")
+            nc.vector.tensor_tensor(
+                k_grouped[g][:, start:end, t : t + 2].rearrange("p (n j) t -> p n j t", j=RUN),
+                pair_rows(pair)[:, :, start:end].rearrange("p t (n j) -> p n j t", j=RUN),
+                runs.unsqueeze(3).to_broadcast([P, (end - start) // RUN, RUN, 2]),
+                MULT,
+            )
 
         def quantise(g, h, start, width):
             cols = slice(start, start + width)
@@ -142,13 +148,38 @@ def tile_attend_pq_lin_bias_kernel(tc, qT, cb, norm, bias, offs, offs2, out):
             nc.vector.tensor_tensor(out_sb[:, cols], banks[i][:], bias_sb[:, cols], ADD)
             nc.sync.dma_start(out[0][:, cols], out_sb[:, cols])
 
-        for pair in range(2 * PASSES):
+        for pair in range(3):
             gather(2 * pair)
             gather(2 * pair + 1)
-            weave(pair)
+            weave_on_gpsimd(pair, 0, QUARTER)
+            weave_on_gpsimd(pair, QUARTER, SHARE[pair])
+            if SHARE[pair] < HALF:
+                weave_on_vector(pair, SHARE[pair], HALF)
+            weave_on_vector(pair, HALF, N)
             if pair == 1:
                 quantise(0, 1, 0, HALF)
                 quantise(0, 0, 0, HALF)
+
+        products = ring[:].rearrange("p s (h c) -> p (s h) c", h=2)[:, 1:3, :]
+        for start in (0, HALF):
+            looked_up = planes[1][2][:].indirect(entries(6, start, HALF))
+            nc.scalar.activation(ring[:, 2, start : start + HALF], looked_up, COPY)
+        nc.vector.tensor_tensor(
+            products[:, 0, :].rearrange("p (n j) -> p n j", j=RUN),
+            ring[:, 2, :HALF].rearrange("p (n j) -> p n j", j=RUN),
+            spread[0][:].rearrange("p j n -> p n j"),
+            MULT,
+        )
+        for start in (0, QUARTER):
+            cols = slice(start, start + QUARTER)
+            looked_up = planes[1][3][:].indirect(entries(7, start, QUARTER))
+            nc.vector.tensor_tensor(products[:, 1, cols], looked_up, norm_sb[:, cols], MULT)
+        nc.scalar.activation(ring[:, 1, HALF:], planes[1][3][:].indirect(entries(7, HALF, HALF)), COPY)
+        for start in (0, QUARTER):
+            cols = slice(start, start + QUARTER)
+            rows = products[:, :, cols].rearrange("p t c -> p c t")
+            nc.gpsimd.tensor_scalar(k_grouped[1][:, cols, 2:], rows, 1.0, 0.0, MULT, ADD)
+        weave_on_vector(3, HALF, N)
 
         q_both = keep.tile([P, PASSES, NQ, PACK], BF16, name="q_both", tag="plane13", align_bytes=64)
         q_grouped = [q_both[:, g] for g in range(PASSES)]

@@ -22,8 +22,7 @@ HALF = N // 2
 QUARTER = N // 4
 RUN = HALF // P
 
-LOADS = [(0, 0), (0, 1), (0, 3), (0, 2), (1, 0), (1, 1), (1, 2), (1, 3)]
-SHARE = [HALF, HALF, HALF]
+LOADS = [(g, t) for g in range(PASSES) for t in (0, 1, 3, 2)]
 
 
 def tile_attend_pq_lin_bias_kernel(tc, qT, cb, norm, bias, offs, offs2, out):
@@ -39,6 +38,7 @@ def tile_attend_pq_lin_bias_kernel(tc, qT, cb, norm, bias, offs, offs2, out):
         norm_runs = keep.tile([P, 2, 2 * RUN], F32, name="norm_runs")
         identity = keep.tile([P, P], F32, name="identity")
         norm_sb = keep.tile([P, HALF], F32, name="norm_sb")
+        norm_gpsimd = keep.tile([P, HALF], F32, name="norm_gpsimd", align_bytes=64)
         bias_sb = keep.tile([P, N], F32, name="bias_sb")
         planes = [
             [keep.tile([P, C], F32, name=f"plane{g}{t}", align_bytes=64) for t in range(PACK)] for g in range(PASSES)
@@ -66,49 +66,34 @@ def tile_attend_pq_lin_bias_kernel(tc, qT, cb, norm, bias, offs, offs2, out):
         nc.sync.dma_start(bias_sb[:], bias)
 
         make_identity(nc, identity[:])
-        for h in range(2):
+        for h in (1, 0):
             for j in range(RUN):
                 column = norm_runs[:, h, j : j + 1]
                 nc.tensor.transpose(spread[h][:, j, :], column.to_broadcast([P, P]), identity[:])
-        nc.scalar.copy(norm_sb[:].rearrange("p (n j) -> p n j", j=RUN), spread[0][:].rearrange("p j n -> p n j"))
+        for copy, tile in ((nc.scalar.copy, norm_gpsimd), (nc.vector.tensor_copy, norm_sb)):
+            copy(tile[:].rearrange("p (n j) -> p n j", j=RUN), spread[1][:].rearrange("p j n -> p n j"))
 
-        ring = keep.tile([P, 3, N], F32, name="ring", tag="norm_runs")
+        rooms = keep.tile([P, 2, 3, HALF], F32, name="rooms", tag="norm_runs")
+        lower, upper = rooms[:, 0, ::-1, :], rooms[:, 1]
 
-        def entries(row, start, width):
-            return lists[LOADS[row][0]][:, start // LIST : (start + width) // LIST]
+        def room(half, row):
+            return half[:, 1 if row % 2 else row % PACK, :]
 
-        def slot(row):
-            return 1 if row % 2 else row % 4
-
-        def gather(row):
+        def looked_up(row, start, width, dtype=F32):
             g, t = LOADS[row]
-            first = row % 2 * HALF
-            for start in range(0, first, QUARTER):
-                window = planes[g][t][:].bitcast(U32).indirect(entries(row, start, QUARTER))
-                nc.vector.tensor_copy(ring[:, slot(row), start : start + QUARTER].bitcast(U32), window)
-            nc.scalar.activation(ring[:, slot(row), first:], planes[g][t][:].indirect(entries(row, first, N - first)), COPY)
+            return planes[g][t][:].bitcast(dtype).indirect(lists[g][:, start // LIST : (start + width) // LIST])
 
-        def pair_rows(pair):
-            if pair == 3:
-                return ring[:, 2:0:-1, :]
-            return ring[:, pair % 2 : pair % 2 + 2, :]
+        def weave_upper(g, start):
+            woven = k_grouped[g][:, HALF + start : HALF + start + QUARTER, 2:]
+            return woven, upper[:, 1:, start : start + QUARTER].rearrange("p t c -> p c t")
 
-        def weave_on_gpsimd(pair, start, end):
+        def weave_lower(pair, start=0, width=HALF):
             g, t = pair // 2, pair % 2 * 2
-            nc.gpsimd.tensor_tensor(
-                k_grouped[g][:, start:end, t : t + 2],
-                pair_rows(pair)[:, :, start:end].rearrange("p t c -> p c t"),
-                norm_sb[:, start:end].unsqueeze(2).to_broadcast([P, end - start, 2]),
-                MULT,
-            )
-
-        def weave_on_vector(pair, start, end):
-            g, t = pair // 2, pair % 2 * 2
-            runs = spread[start // HALF][:, :, start % HALF // RUN :].rearrange("p j n -> p n j")
+            runs = spread[0][:, :, start // RUN : (start + width) // RUN].rearrange("p j n -> p n j")
             nc.vector.tensor_tensor(
-                k_grouped[g][:, start:end, t : t + 2].rearrange("p (n j) t -> p n j t", j=RUN),
-                pair_rows(pair)[:, :, start:end].rearrange("p t (n j) -> p n j t", j=RUN),
-                runs.unsqueeze(3).to_broadcast([P, (end - start) // RUN, RUN, 2]),
+                k_grouped[g][:, start : start + width, t : t + 2].rearrange("p (n j) t -> p n j t", j=RUN),
+                lower[:, pair % 2 : pair % 2 + 2, start : start + width].rearrange("p t (n j) -> p n j t", j=RUN),
+                runs.unsqueeze(3).to_broadcast([P, width // RUN, RUN, 2]),
                 MULT,
             )
 
@@ -120,14 +105,12 @@ def tile_attend_pq_lin_bias_kernel(tc, qT, cb, norm, bias, offs, offs2, out):
                 in_=k_grouped[g][:, h * HALF + start : h * HALF + start + width, :].rearrange("p c t -> p (c t)"),
             )
 
-        def round_q(g):
-            nc.scalar.copy(q_grouped[g], q_raw[g][:].rearrange("p t q -> p q t"))
 
         def quantise_q(g):
             nc.vector.quantize_mx(
                 out=q_codes[g][:].bitcast(FP8X4),
                 scales=q_scales[g][:],
-                in_=q_grouped[g].rearrange("p q t -> p (q t)"),
+                in_=q_grouped[g][:].rearrange("p q t -> p (q t)"),
             )
 
         def multiply(g, i):
@@ -148,56 +131,62 @@ def tile_attend_pq_lin_bias_kernel(tc, qT, cb, norm, bias, offs, offs2, out):
             nc.vector.tensor_tensor(out_sb[:, cols], banks[i][:], bias_sb[:, cols], ADD)
             nc.sync.dma_start(out[0][:, cols], out_sb[:, cols])
 
-        for pair in range(3):
-            gather(2 * pair)
-            gather(2 * pair + 1)
-            weave_on_gpsimd(pair, 0, QUARTER)
-            weave_on_gpsimd(pair, QUARTER, SHARE[pair])
-            if SHARE[pair] < HALF:
-                weave_on_vector(pair, SHARE[pair], HALF)
-            weave_on_vector(pair, HALF, N)
-            if pair == 1:
-                quantise(0, 1, 0, HALF)
+        for g in range(PASSES):
+            row = PACK * g
+            both_halves = rooms[:].rearrange("p h s c -> p (h s c)")[:, 2 * HALF : 4 * HALF]
+            nc.scalar.activation(both_halves, looked_up(row, 0, N), COPY)
+            for start in (0, QUARTER):
+                words = room(upper, row + 1)[:, start : start + QUARTER].bitcast(U32)
+                nc.vector.tensor_copy(words, looked_up(row + 1, HALF + start, QUARTER, U32))
+            nc.scalar.activation(room(lower, row + 1), looked_up(row + 1, 0, HALF), COPY)
+            for start in (0, QUARTER):
+                cols = slice(start, start + QUARTER)
+                nc.gpsimd.tensor_tensor(
+                    k_grouped[g][:, HALF + start : HALF + start + QUARTER, :2],
+                    upper[:, :2, cols].rearrange("p t c -> p c t"),
+                    norm_gpsimd[:, cols].unsqueeze(2).to_broadcast([P, QUARTER, 2]),
+                    MULT,
+                )
+            weave_lower(2 * g)
+
+            nc.scalar.activation(room(upper, row + 2), looked_up(row + 2, HALF, HALF), COPY)
+            nc.scalar.activation(room(lower, row + 2), looked_up(row + 2, 0, HALF), COPY)
+            in_runs = room(upper, row + 2).rearrange("p (n j) -> p n j", j=RUN)
+            nc.vector.tensor_tensor(in_runs, in_runs, spread[1][:].rearrange("p j n -> p n j"), MULT)
+            width = (QUARTER, HALF)[g]
+            for start in range(0, HALF, width):
+                cols = slice(start, start + width)
+                gathered = looked_up(row + 3, HALF + start, width)
+                nc.vector.tensor_tensor(room(upper, row + 3)[:, cols], gathered, norm_sb[:, cols], MULT)
+            nc.scalar.activation(room(lower, row + 3), looked_up(row + 3, 0, HALF), COPY)
+            if g == 0:
+                for start in (0, QUARTER):
+                    nc.gpsimd.tensor_scalar(*weave_upper(0, start), 1.0, 0.0, MULT, ADD)
+                weave_lower(1)
                 quantise(0, 0, 0, HALF)
+                quantise(0, 1, 0, HALF)
 
-        products = ring[:].rearrange("p s (h c) -> p (s h) c", h=2)[:, 1:3, :]
-        for start in (0, HALF):
-            looked_up = planes[1][2][:].indirect(entries(6, start, HALF))
-            nc.scalar.activation(ring[:, 2, start : start + HALF], looked_up, COPY)
-        nc.vector.tensor_tensor(
-            products[:, 0, :].rearrange("p (n j) -> p n j", j=RUN),
-            ring[:, 2, :HALF].rearrange("p (n j) -> p n j", j=RUN),
-            spread[0][:].rearrange("p j n -> p n j"),
-            MULT,
-        )
-        for start in (0, QUARTER):
-            cols = slice(start, start + QUARTER)
-            looked_up = planes[1][3][:].indirect(entries(7, start, QUARTER))
-            nc.vector.tensor_tensor(products[:, 1, cols], looked_up, norm_sb[:, cols], MULT)
-        nc.scalar.activation(ring[:, 1, HALF:], planes[1][3][:].indirect(entries(7, HALF, HALF)), COPY)
-        for start in (0, QUARTER):
-            cols = slice(start, start + QUARTER)
-            rows = products[:, :, cols].rearrange("p t c -> p c t")
-            nc.gpsimd.tensor_scalar(k_grouped[1][:, cols, 2:], rows, 1.0, 0.0, MULT, ADD)
-        weave_on_vector(3, HALF, N)
-
-        q_both = keep.tile([P, PASSES, NQ, PACK], BF16, name="q_both", tag="plane13", align_bytes=64)
-        q_grouped = [q_both[:, g] for g in range(PASSES)]
-        round_q(0)
-        round_q(1)
+        q_grouped = [
+            keep.tile([P, NQ, PACK], BF16, name=f"q_grouped{g}", tag=tag, align_bytes=64)
+            for g, tag in enumerate(("norm_gpsimd", "plane12"))
+        ]
+        nc.gpsimd.tensor_scalar(q_grouped[0][:], q_raw[0][:].rearrange("p t q -> p q t"), 1.0, 0.0, MULT, ADD)
+        nc.scalar.copy(*weave_upper(1, 0))
+        nc.scalar.copy(q_grouped[1][:], q_raw[1][:].rearrange("p t q -> p q t"))
+        nc.scalar.copy(*weave_upper(1, QUARTER))
+        weave_lower(3, 0, QUARTER)
         quantise_q(0)
-        quantise_q(1)
-        quantise(1, 1, 0, HALF)
-        for i in (2, 3):
+        for i in (2, 0, 1, 3):
             multiply(0, i)
+        weave_lower(3, QUARTER, QUARTER)
+        quantise(1, 1, 0, QUARTER)
+        quantise_q(1)
         multiply(1, 2)
-        multiply(1, 3)
-        quantise(1, 0, 0, QUARTER)
-        multiply(0, 0)
+        quantise(1, 0, 0, HALF)
         multiply(1, 0)
-        finish(2)
-        quantise(1, 0, QUARTER, QUARTER)
-        multiply(0, 1)
         multiply(1, 1)
-        for i in (3, 0, 1):
+        finish(2)
+        quantise(1, 1, QUARTER, QUARTER)
+        multiply(1, 3)
+        for i in (0, 1, 3):
             finish(i)

@@ -7,6 +7,7 @@ FLOPS = 2 * NQ * D * N
 F32 = mybir.dt.float32
 BF16 = mybir.dt.bfloat16
 U32 = mybir.dt.uint32
+I32 = mybir.dt.int32
 U16 = mybir.dt.uint16
 U8 = mybir.dt.uint8
 FP8X4 = mybir.dt.float8_e4m3fn_x4
@@ -48,6 +49,8 @@ def tile_attend_pq_lin_bias_kernel(tc, qT, cb, norm, bias, offs, offs2, out):
         q_scales = [keep.tile([P, NQ], U8, name=f"q_scales{g}", align_bytes=64) for g in range(PASSES)]
         halves = [(g, h) for g in range(PASSES) for h in range(2)]
         k_grouped = [keep.tile([P, N, PACK], BF16, name=f"k_grouped{g}", align_bytes=64) for g in range(PASSES)]
+        pairs = keep.tile([P, 2, HALF, 2], BF16, name="pairs", align_bytes=64)
+        k_lower = [keep.tile([P, QUARTER, PACK], BF16, name=f"k_lower{i}", align_bytes=64) for i in range(2)]
         k_codes = {gh: keep.tile([P, HALF], U32, name="k_codes%d%d" % gh, align_bytes=64) for gh in halves}
         k_scales = {gh: keep.tile([P, HALF], U8, name="k_scales%d%d" % gh, align_bytes=64) for gh in halves}
         out_sb = keep.tile([P, N], F32, name="out_sb")
@@ -90,19 +93,29 @@ def tile_attend_pq_lin_bias_kernel(tc, qT, cb, norm, bias, offs, offs2, out):
         def weave_lower(pair, start=0, width=HALF):
             g, t = pair // 2, pair % 2 * 2
             runs = spread[0][:, :, start // RUN : (start + width) // RUN].rearrange("p j n -> p n j")
+            woven = pairs[:, t // 2, start : start + width, :] if g else k_grouped[g][:, start : start + width, t : t + 2]
             nc.vector.tensor_tensor(
-                k_grouped[g][:, start : start + width, t : t + 2].rearrange("p (n j) t -> p n j t", j=RUN),
+                woven.rearrange("p (n j) t -> p n j t", j=RUN),
                 lower[:, pair % 2 : pair % 2 + 2, start : start + width].rearrange("p t (n j) -> p n j t", j=RUN),
                 runs.unsqueeze(3).to_broadcast([P, width // RUN, RUN, 2]),
                 MULT,
             )
 
+        def merge(copy, dtype, i):
+            words = pairs[:].rearrange("p u c t -> p u (c t)").bitcast(dtype)[:, :, i * QUARTER : (i + 1) * QUARTER]
+            merged = k_lower[i][:].rearrange("p c t -> p (c t)").bitcast(dtype).rearrange("p (c u) -> p c u", u=2)
+            copy(merged, words.rearrange("p u c -> p c u"))
+
         def quantise(g, h, start, width):
             cols = slice(start, start + width)
+            if (g, h) == (1, 0):
+                grouped = k_lower[start // QUARTER][:]
+            else:
+                grouped = k_grouped[g][:, h * HALF + start : h * HALF + start + width, :]
             nc.vector.quantize_mx(
                 out=k_codes[g, h][:, cols].bitcast(FP8X4),
                 scales=k_scales[g, h][:, cols],
-                in_=k_grouped[g][:, h * HALF + start : h * HALF + start + width, :].rearrange("p c t -> p (c t)"),
+                in_=grouped.rearrange("p c t -> p (c t)"),
             )
 
 
@@ -173,18 +186,22 @@ def tile_attend_pq_lin_bias_kernel(tc, qT, cb, norm, bias, offs, offs2, out):
         nc.gpsimd.tensor_scalar(q_grouped[0][:], q_raw[0][:].rearrange("p t q -> p q t"), 1.0, 0.0, MULT, ADD)
         nc.scalar.copy(*weave_upper(1, 0))
         nc.scalar.copy(q_grouped[1][:], q_raw[1][:].rearrange("p t q -> p q t"))
-        nc.scalar.copy(*weave_upper(1, QUARTER))
         weave_lower(3, 0, QUARTER)
-        quantise_q(0)
-        for i in (2, 0, 1, 3):
-            multiply(0, i)
         weave_lower(3, QUARTER, QUARTER)
-        quantise(1, 1, 0, QUARTER)
+        merge(nc.scalar.copy, U32, 1)
+        nc.scalar.copy(*weave_upper(1, QUARTER))
+        quantise_q(0)
+        merge(nc.vector.tensor_copy, I32, 0)
         quantise_q(1)
+        quantise(1, 1, 0, QUARTER)
+        for i in (2, 0):
+            multiply(0, i)
         multiply(1, 2)
-        quantise(1, 0, 0, HALF)
-        multiply(1, 0)
-        multiply(1, 1)
+        multiply(0, 1)
+        for i in (0, 1):
+            quantise(1, 0, i * QUARTER, QUARTER)
+            multiply(1, i)
+        multiply(0, 3)
         finish(2)
         quantise(1, 1, QUARTER, QUARTER)
         multiply(1, 3)

@@ -39,7 +39,6 @@ def tile_attend_pq_lin_bias_kernel(tc, qT, cb, norm, bias, offs, offs2, out):
         norm_runs = keep.tile([P, 2, 2 * RUN], F32, name="norm_runs")
         identity = keep.tile([P, P], F32, name="identity")
         norm_sb = keep.tile([P, HALF], F32, name="norm_sb")
-        norm_gpsimd = keep.tile([P, HALF], F32, name="norm_gpsimd", align_bytes=64)
         bias_sb = keep.tile([P, N], F32, name="bias_sb")
         planes = [
             [keep.tile([P, C], F32, name=f"plane{g}{t}", align_bytes=64) for t in range(PACK)] for g in range(PASSES)
@@ -73,8 +72,7 @@ def tile_attend_pq_lin_bias_kernel(tc, qT, cb, norm, bias, offs, offs2, out):
             for j in range(RUN):
                 column = norm_runs[:, h, j : j + 1]
                 nc.tensor.transpose(spread[h][:, j, :], column.to_broadcast([P, P]), identity[:])
-        for copy, tile in ((nc.scalar.copy, norm_gpsimd), (nc.vector.tensor_copy, norm_sb)):
-            copy(tile[:].rearrange("p (n j) -> p n j", j=RUN), spread[1][:].rearrange("p j n -> p n j"))
+        nc.scalar.copy(norm_sb[:].rearrange("p (n j) -> p n j", j=RUN), spread[1][:].rearrange("p j n -> p n j"))
 
         rooms = keep.tile([P, 2, 3, HALF], F32, name="rooms", tag="norm_runs")
         lower, upper = rooms[:, 0, ::-1, :], rooms[:, 1]
@@ -123,7 +121,7 @@ def tile_attend_pq_lin_bias_kernel(tc, qT, cb, norm, bias, offs, offs2, out):
             nc.vector.quantize_mx(
                 out=q_codes[g][:].bitcast(FP8X4),
                 scales=q_scales[g][:],
-                in_=q_grouped[g][:].rearrange("p q t -> p (q t)"),
+                in_=q_grouped[g].rearrange("p q t -> p (q t)"),
             )
 
         def multiply(g, i):
@@ -157,7 +155,7 @@ def tile_attend_pq_lin_bias_kernel(tc, qT, cb, norm, bias, offs, offs2, out):
                 nc.gpsimd.tensor_tensor(
                     k_grouped[g][:, HALF + start : HALF + start + QUARTER, :2],
                     upper[:, :2, cols].rearrange("p t c -> p c t"),
-                    norm_gpsimd[:, cols].unsqueeze(2).to_broadcast([P, QUARTER, 2]),
+                    norm_sb[:, cols].unsqueeze(2).to_broadcast([P, QUARTER, 2]),
                     MULT,
                 )
             weave_lower(2 * g)
@@ -179,15 +177,17 @@ def tile_attend_pq_lin_bias_kernel(tc, qT, cb, norm, bias, offs, offs2, out):
                 quantise(0, 0, 0, HALF)
                 quantise(0, 1, 0, HALF)
 
-        q_grouped = [
+        q_tiles = [
             keep.tile([P, NQ, PACK], BF16, name=f"q_grouped{g}", tag=tag, align_bytes=64)
-            for g, tag in enumerate(("norm_gpsimd", "plane12"))
+            for g, tag in enumerate(("plane13", "plane12"))
         ]
-        nc.gpsimd.tensor_scalar(q_grouped[0][:], q_raw[0][:].rearrange("p t q -> p q t"), 1.0, 0.0, MULT, ADD)
-        nc.scalar.copy(*weave_upper(1, 0))
-        nc.scalar.copy(q_grouped[1][:], q_raw[1][:].rearrange("p t q -> p q t"))
-        weave_lower(3, 0, QUARTER)
-        weave_lower(3, QUARTER, QUARTER)
+        q_grouped = [tile[:] for tile in q_tiles]
+        nc.gpsimd.tensor_scalar(*weave_upper(1, 0), 1.0, 0.0, MULT, ADD)
+        for g in range(PASSES):
+            nc.scalar.copy(
+                q_grouped[g].rearrange("p (c i) t -> p c t i", i=4), q_raw[g][:].rearrange("p t (c i) -> p c t i", i=4)
+            )
+        weave_lower(3)
         merge(nc.scalar.copy, U32, 1)
         nc.scalar.copy(*weave_upper(1, QUARTER))
         quantise_q(0)

@@ -84,9 +84,9 @@ def tile_attend_pq_lin_bias_kernel(tc, qT, cb, norm, bias, offs, offs2, out):
             g, t = LOADS[row]
             return planes[g][t][:].bitcast(dtype).indirect(lists[g][:, start // LIST : (start + width) // LIST])
 
-        def weave_upper(g, start):
-            woven = k_grouped[g][:, HALF + start : HALF + start + QUARTER, 2:]
-            return woven, upper[:, 1:, start : start + QUARTER].rearrange("p t c -> p c t")
+        def weave_upper(g, start, width=QUARTER):
+            woven = k_grouped[g][:, HALF + start : HALF + start + width, 2:]
+            return woven, upper[:, 1:, start : start + width].rearrange("p t c -> p c t")
 
         def weave_lower(pair, start=0, width=HALF):
             g, t = pair // 2, pair % 2 * 2
@@ -182,26 +182,26 @@ def tile_attend_pq_lin_bias_kernel(tc, qT, cb, norm, bias, offs, offs2, out):
             for g, tag in enumerate(("plane13", "plane12"))
         ]
         q_grouped = [tile[:] for tile in q_tiles]
-        nc.gpsimd.tensor_scalar(*weave_upper(1, 0), 1.0, 0.0, MULT, ADD)
+        nc.gpsimd.tensor_scalar(*weave_upper(1, 0, 192), 1.0, 0.0, MULT, ADD)
         for g in range(PASSES):
             nc.scalar.copy(
                 q_grouped[g].rearrange("p (c i) t -> p c t i", i=4), q_raw[g][:].rearrange("p t (c i) -> p c t i", i=4)
             )
-        weave_lower(3)
+        nc.scalar.copy(*weave_upper(1, 192, 64))
+        weave_lower(3, 0, 352)
+        quantise_q(0)
+        weave_lower(3, 352, 160)
         merge(nc.scalar.copy, U32, 1)
         nc.scalar.copy(*weave_upper(1, QUARTER))
-        quantise_q(0)
         merge(nc.vector.tensor_copy, I32, 0)
         quantise_q(1)
         quantise(1, 1, 0, QUARTER)
-        for i in (2, 0):
+        for i in (2, 0, 1, 3):
             multiply(0, i)
         multiply(1, 2)
-        multiply(0, 1)
         for i in (0, 1):
             quantise(1, 0, i * QUARTER, QUARTER)
             multiply(1, i)
-        multiply(0, 3)
         finish(2)
         quantise(1, 1, QUARTER, QUARTER)
         multiply(1, 3)

@@ -24,6 +24,7 @@ QUARTER = N // 4
 RUN = HALF // P
 
 LOADS = [(g, t) for g in range(PASSES) for t in (0, 1, 3, 2)]
+SEVENTH = 384
 
 
 def tile_attend_pq_lin_bias_kernel(tc, qT, cb, norm, bias, offs, offs2, out):
@@ -74,8 +75,10 @@ def tile_attend_pq_lin_bias_kernel(tc, qT, cb, norm, bias, offs, offs2, out):
                 nc.tensor.transpose(spread[h][:, j, :], column.to_broadcast([P, P]), identity[:])
         nc.scalar.copy(norm_sb[:].rearrange("p (n j) -> p n j", j=RUN), spread[1][:].rearrange("p j n -> p n j"))
 
-        rooms = keep.tile([P, 2, 3, HALF], F32, name="rooms", tag="norm_runs")
-        lower, upper = rooms[:, 0, ::-1, :], rooms[:, 1]
+        rooms = keep.tile([P, 7, HALF], F32, name="rooms", tag="norm_runs")
+        lower_pairs = [rooms[:, 3:1:-1, :], rooms[:, 2::-2, :]]
+        upper = rooms[:, 4:, :]
+        flat = rooms[:].rearrange("p s c -> p (s c)")
 
         def room(half, row):
             return half[:, 1 if row % 2 else row % PACK, :]
@@ -94,7 +97,7 @@ def tile_attend_pq_lin_bias_kernel(tc, qT, cb, norm, bias, offs, offs2, out):
             woven = pairs[:, t // 2, start : start + width, :] if g else k_grouped[g][:, start : start + width, t : t + 2]
             nc.vector.tensor_tensor(
                 woven.rearrange("p (n j) t -> p n j t", j=RUN),
-                lower[:, pair % 2 : pair % 2 + 2, start : start + width].rearrange("p t (n j) -> p n j t", j=RUN),
+                lower_pairs[pair % 2][:, :, start : start + width].rearrange("p t (n j) -> p n j t", j=RUN),
                 runs.unsqueeze(3).to_broadcast([P, width // RUN, RUN, 2]),
                 MULT,
             )
@@ -144,12 +147,12 @@ def tile_attend_pq_lin_bias_kernel(tc, qT, cb, norm, bias, offs, offs2, out):
 
         for g in range(PASSES):
             row = PACK * g
-            both_halves = rooms[:].rearrange("p h s c -> p (h s c)")[:, 2 * HALF : 4 * HALF]
+            both_halves = flat[:, 3 * HALF : 5 * HALF]
             nc.scalar.activation(both_halves, looked_up(row, 0, N), COPY)
             for start in (0, QUARTER):
                 words = room(upper, row + 1)[:, start : start + QUARTER].bitcast(U32)
                 nc.vector.tensor_copy(words, looked_up(row + 1, HALF + start, QUARTER, U32))
-            nc.scalar.activation(room(lower, row + 1), looked_up(row + 1, 0, HALF), COPY)
+            nc.scalar.activation(rooms[:, 2, :], looked_up(row + 1, 0, HALF), COPY)
             for start in (0, QUARTER):
                 cols = slice(start, start + QUARTER)
                 nc.gpsimd.tensor_tensor(
@@ -160,16 +163,24 @@ def tile_attend_pq_lin_bias_kernel(tc, qT, cb, norm, bias, offs, offs2, out):
                 )
             weave_lower(2 * g)
 
-            nc.scalar.activation(room(upper, row + 2), looked_up(row + 2, HALF, HALF), COPY)
-            nc.scalar.activation(room(lower, row + 2), looked_up(row + 2, 0, HALF), COPY)
-            in_runs = room(upper, row + 2).rearrange("p (n j) -> p n j", j=RUN)
-            nc.vector.tensor_tensor(in_runs, in_runs, spread[1][:].rearrange("p j n -> p n j"), MULT)
+            if g == 0:
+                nc.scalar.activation(rooms[:, 1, :], looked_up(row + 2, HALF, HALF), COPY)
+                nc.scalar.activation(rooms[:, 0, :], looked_up(row + 2, 0, HALF), COPY)
+            else:
+                nc.scalar.activation(flat[:, SEVENTH:N], looked_up(row + 2, SEVENTH, N - SEVENTH), COPY)
+                nc.vector.tensor_copy(flat[:, :SEVENTH].bitcast(U32), looked_up(row + 2, 0, SEVENTH, U32))
+            nc.vector.tensor_tensor(
+                room(upper, row + 2).rearrange("p (n j) -> p n j", j=RUN),
+                rooms[:, 1, :].rearrange("p (n j) -> p n j", j=RUN),
+                spread[1][:].rearrange("p j n -> p n j"),
+                MULT,
+            )
             width = (QUARTER, HALF)[g]
             for start in range(0, HALF, width):
                 cols = slice(start, start + width)
                 gathered = looked_up(row + 3, HALF + start, width)
                 nc.vector.tensor_tensor(room(upper, row + 3)[:, cols], gathered, norm_sb[:, cols], MULT)
-            nc.scalar.activation(room(lower, row + 3), looked_up(row + 3, 0, HALF), COPY)
+            nc.scalar.activation(rooms[:, 2, :], looked_up(row + 3, 0, HALF), COPY)
             if g == 0:
                 for start in (0, QUARTER):
                     nc.gpsimd.tensor_scalar(*weave_upper(0, start), 1.0, 0.0, MULT, ADD)

@@ -23,8 +23,10 @@ HALF = N // 2
 QUARTER = N // 4
 RUN = HALF // P
 
-LOADS = [(g, t) for g in range(PASSES) for t in (0, 1, 3, 2)]
-SEVENTH = 384
+LOAD_ORDER = (0, 1, 3, 2)
+SCALAR_SEVENTH = 640
+GPSIMD_WEAVE = 160
+FIRST_CUT = 384
 
 
 def tile_attend_pq_lin_bias_kernel(tc, qT, cb, norm, bias, offs, offs2, out):
@@ -34,36 +36,43 @@ def tile_attend_pq_lin_bias_kernel(tc, qT, cb, norm, bias, offs, offs2, out):
 
     with (
         tc.tile_pool(name="keep", bufs=1) as keep,
+        tc.tile_pool(name="late", bufs=1) as late,
         tc.psum_pool(name="psum", bufs=1) as psum,
     ):
         lists = [keep.tile([P, N // LIST], U16, name=f"list{g}") for g in range(PASSES)]
         norm_runs = keep.tile([P, 2, 2 * RUN], F32, name="norm_runs")
         identity = keep.tile([P, P], F32, name="identity")
-        norm_sb = keep.tile([P, HALF], F32, name="norm_sb")
+        norm_upper = keep.tile([P, HALF], F32, name="norm_upper")
         bias_sb = keep.tile([P, N], F32, name="bias_sb")
         planes = [
             [keep.tile([P, C], F32, name=f"plane{g}{t}", align_bytes=64) for t in range(PACK)] for g in range(PASSES)
         ]
-        q_raw = [keep.tile([P, PACK, NQ], F32, name=f"q_raw{g}", align_bytes=64) for g in range(PASSES)]
+        q_raw = [
+            keep.tile([P, PACK, NQ], F32, name="q_raw0", align_bytes=64),
+            late.tile([P, PACK, NQ], F32, name="q_raw1", align_bytes=64, offset=1024),
+        ]
         q_codes = [keep.tile([P, NQ], U32, name=f"q_codes{g}", align_bytes=64) for g in range(PASSES)]
         q_scales = [keep.tile([P, NQ], U8, name=f"q_scales{g}", align_bytes=64) for g in range(PASSES)]
-        halves = [(g, h) for g in range(PASSES) for h in range(2)]
-        k_grouped = [keep.tile([P, N, PACK], BF16, name=f"k_grouped{g}", align_bytes=64) for g in range(PASSES)]
+        k_first = keep.tile([P, N, PACK], BF16, name="k_first", align_bytes=64)
+        k_second = [
+            late.tile([P, QUARTER, PACK], BF16, name=f"k_second{i}", align_bytes=64, offset=2048 * i) for i in range(2)
+        ] + [keep.tile([P, QUARTER, PACK], BF16, name=f"k_second{i}", align_bytes=64) for i in (2, 3)]
         pairs = keep.tile([P, 2, HALF, 2], BF16, name="pairs", align_bytes=64)
-        k_lower = [keep.tile([P, QUARTER, PACK], BF16, name=f"k_lower{i}", align_bytes=64) for i in range(2)]
-        k_codes = {gh: keep.tile([P, HALF], U32, name="k_codes%d%d" % gh, align_bytes=64) for gh in halves}
-        k_scales = {gh: keep.tile([P, HALF], U8, name="k_scales%d%d" % gh, align_bytes=64) for gh in halves}
-        out_sb = keep.tile([P, N], F32, name="out_sb")
+        first_codes = keep.tile([P, N], U32, name="first_codes", align_bytes=64)
+        first_scales = keep.tile([P, N], U8, name="first_scales", align_bytes=64)
+        second_codes = [keep.tile([P, QUARTER], U32, name=f"second_codes{i}", align_bytes=64) for i in range(4)]
+        second_scales = [keep.tile([P, QUARTER], U8, name=f"second_scales{i}", align_bytes=64) for i in range(4)]
         banks = [psum.tile([P, QUARTER], F32, name=f"bank{i}") for i in range(4)]
         spread = [psum.tile([P, RUN, P], F32, name=f"spread{h}") for h in range(2)]
 
         nc.sync.dma_start(norm_runs[:, :, :RUN], norm[0].rearrange("(h p j) -> p h j", h=2, j=RUN))
-        for row, (g, t) in enumerate(LOADS):
-            if row == PACK:
-                nc.sync.dma_start(lists[1][:], offs2)
-            nc.sync.dma_start(planes[g][t][:], cb_planes[g, t])
-            if row == 0:
-                nc.sync.dma_start(lists[0][:], offs)
+        for g in range(PASSES):
+            for place, t in enumerate(LOAD_ORDER):
+                if (g, place) == (1, 0):
+                    nc.sync.dma_start(lists[1][:], offs2)
+                nc.sync.dma_start(planes[g][t][:], cb_planes[g, t])
+                if (g, place) == (0, 0):
+                    nc.sync.dma_start(lists[0][:], offs)
         for g in range(PASSES):
             nc.sync.dma_start(q_raw[g][:], q_rows[g])
         nc.sync.dma_start(bias_sb[:], bias)
@@ -73,69 +82,54 @@ def tile_attend_pq_lin_bias_kernel(tc, qT, cb, norm, bias, offs, offs2, out):
             for j in range(RUN):
                 column = norm_runs[:, h, j : j + 1]
                 nc.tensor.transpose(spread[h][:, j, :], column.to_broadcast([P, P]), identity[:])
-        nc.scalar.copy(norm_sb[:].rearrange("p (n j) -> p n j", j=RUN), spread[1][:].rearrange("p j n -> p n j"))
+        nc.scalar.copy(norm_upper[:].rearrange("p (n j) -> p n j", j=RUN), spread[1][:].rearrange("p j n -> p n j"))
 
         rooms = keep.tile([P, 7, HALF], F32, name="rooms", tag="norm_runs")
-        lower_pairs = [rooms[:, 3:1:-1, :], rooms[:, 2::-2, :]]
-        upper = rooms[:, 4:, :]
         flat = rooms[:].rearrange("p s c -> p (s c)")
 
-        def room(half, row):
-            return half[:, 1 if row % 2 else row % PACK, :]
-
-        def looked_up(row, start, width, dtype=F32):
-            g, t = LOADS[row]
+        def looked_up(g, t, start, width, dtype=F32):
             return planes[g][t][:].bitcast(dtype).indirect(lists[g][:, start // LIST : (start + width) // LIST])
 
-        def weave_upper(g, start, width=QUARTER):
-            woven = k_grouped[g][:, HALF + start : HALF + start + width, 2:]
-            return woven, upper[:, 1:, start : start + width].rearrange("p t c -> p c t")
+        def spread_norm(h, start, width):
+            return spread[h][:, :, start // RUN : (start + width) // RUN].rearrange("p j n -> p n j")
 
-        def weave_lower(pair, start=0, width=HALF):
-            g, t = pair // 2, pair % 2 * 2
-            runs = spread[0][:, :, start // RUN : (start + width) // RUN].rearrange("p j n -> p n j")
-            woven = pairs[:, t // 2, start : start + width, :] if g else k_grouped[g][:, start : start + width, t : t + 2]
+        def multiply_lower(woven, rows, start, width):
             nc.vector.tensor_tensor(
                 woven.rearrange("p (n j) t -> p n j t", j=RUN),
-                lower_pairs[pair % 2][:, :, start : start + width].rearrange("p t (n j) -> p n j t", j=RUN),
-                runs.unsqueeze(3).to_broadcast([P, width // RUN, RUN, 2]),
+                rows[:, :, start : start + width].rearrange("p t (n j) -> p n j t", j=RUN),
+                spread_norm(0, start, width).unsqueeze(3).to_broadcast([P, width // RUN, RUN, 2]),
                 MULT,
             )
 
-        def merge(copy, dtype, i):
-            words = pairs[:].rearrange("p u c t -> p u (c t)").bitcast(dtype)[:, :, i * QUARTER : (i + 1) * QUARTER]
-            merged = k_lower[i][:].rearrange("p c t -> p (c t)").bitcast(dtype).rearrange("p (c u) -> p c u", u=2)
-            copy(merged, words.rearrange("p u c -> p c u"))
+        def upper_place(g, start, width):
+            if g == 0:
+                return k_first[:, HALF + start : HALF + start + width, :]
+            i, col = divmod(start, QUARTER)
+            return k_second[2 + i][:, col : col + width, :]
 
-        def quantise(g, h, start, width):
-            cols = slice(start, start + width)
-            if (g, h) == (1, 0):
-                grouped = k_lower[start // QUARTER][:]
-            else:
-                grouped = k_grouped[g][:, h * HALF + start : h * HALF + start + width, :]
-            nc.vector.quantize_mx(
-                out=k_codes[g, h][:, cols].bitcast(FP8X4),
-                scales=k_scales[g, h][:, cols],
-                in_=grouped.rearrange("p c t -> p (c t)"),
-            )
+        def weave(g, start, width):
+            return upper_place(g, start, width)[:, :, 2:], rooms[:, 5:, start : start + width].rearrange("p t c -> p c t")
 
+        def merge(copy, dtype, start, width):
+            words = pairs[:].rearrange("p u c t -> p u (c t)").bitcast(dtype)[:, :, start : start + width]
+            i, col = divmod(start, QUARTER)
+            merged = k_second[i][:, col : col + width, :].rearrange("p c t -> p (c t)").bitcast(dtype)
+            copy(merged.rearrange("p (c u) -> p c u", u=2), words.rearrange("p u c -> p c u"))
 
-        def quantise_q(g):
-            nc.vector.quantize_mx(
-                out=q_codes[g][:].bitcast(FP8X4),
-                scales=q_scales[g][:],
-                in_=q_grouped[g].rearrange("p q t -> p (q t)"),
-            )
+        def quantise(codes, scales, grouped):
+            nc.vector.quantize_mx(out=codes.bitcast(FP8X4), scales=scales, in_=grouped.rearrange("p c t -> p (c t)"))
 
-        def multiply(g, i):
-            h, first = divmod(i * QUARTER, HALF)
-            cols = slice(first, first + QUARTER)
+        def quantise_second(i):
+            quantise(second_codes[i][:], second_scales[i][:], k_second[i][:])
+
+        def matmul(g, i):
+            cols = slice(i * QUARTER, (i + 1) * QUARTER)
             nc.tensor.matmul_mx(
                 out=banks[i][:],
                 lhsT=q_codes[g][:].bitcast(FP8X4),
                 lhsT_scale=q_scales[g][:],
-                rhs=k_codes[g, h][:, cols].bitcast(FP8X4),
-                rhs_scale=k_scales[g, h][:, cols],
+                rhs=(second_codes[i][:] if g else first_codes[:, cols]).bitcast(FP8X4),
+                rhs_scale=second_scales[i][:] if g else first_scales[:, cols],
                 start=(g == 0),
                 stop=(g == PASSES - 1),
             )
@@ -145,76 +139,85 @@ def tile_attend_pq_lin_bias_kernel(tc, qT, cb, norm, bias, offs, offs2, out):
             nc.vector.tensor_tensor(out_sb[:, cols], banks[i][:], bias_sb[:, cols], ADD)
             nc.sync.dma_start(out[0][:, cols], out_sb[:, cols])
 
-        for g in range(PASSES):
-            row = PACK * g
-            both_halves = flat[:, 3 * HALF : 5 * HALF]
-            nc.scalar.activation(both_halves, looked_up(row, 0, N), COPY)
+        def first_pair(g):
+            nc.scalar.activation(flat[:, 3 * HALF : 5 * HALF], looked_up(g, 0, 0, N), COPY)
             for start in (0, QUARTER):
-                words = room(upper, row + 1)[:, start : start + QUARTER].bitcast(U32)
-                nc.vector.tensor_copy(words, looked_up(row + 1, HALF + start, QUARTER, U32))
-            nc.scalar.activation(rooms[:, 2, :], looked_up(row + 1, 0, HALF), COPY)
+                words = rooms[:, 5, start : start + QUARTER].bitcast(U32)
+                nc.vector.tensor_copy(words, looked_up(g, 1, HALF + start, QUARTER, U32))
+            nc.scalar.activation(rooms[:, 2, :], looked_up(g, 1, 0, HALF), COPY)
             for start in (0, QUARTER):
                 cols = slice(start, start + QUARTER)
                 nc.gpsimd.tensor_tensor(
-                    k_grouped[g][:, HALF + start : HALF + start + QUARTER, :2],
-                    upper[:, :2, cols].rearrange("p t c -> p c t"),
-                    norm_sb[:, cols].unsqueeze(2).to_broadcast([P, QUARTER, 2]),
+                    upper_place(g, start, QUARTER)[:, :, :2],
+                    rooms[:, 4:6, cols].rearrange("p t c -> p c t"),
+                    norm_upper[:, cols].unsqueeze(2).to_broadcast([P, QUARTER, 2]),
                     MULT,
                 )
-            weave_lower(2 * g)
+            multiply_lower(pairs[:, 0, :, :] if g else k_first[:, :HALF, :2], rooms[:, 3:1:-1, :], 0, HALF)
 
-            if g == 0:
-                nc.scalar.activation(rooms[:, 1, :], looked_up(row + 2, HALF, HALF), COPY)
-                nc.scalar.activation(rooms[:, 0, :], looked_up(row + 2, 0, HALF), COPY)
-            else:
-                nc.scalar.activation(flat[:, SEVENTH:N], looked_up(row + 2, SEVENTH, N - SEVENTH), COPY)
-                nc.vector.tensor_copy(flat[:, :SEVENTH].bitcast(U32), looked_up(row + 2, 0, SEVENTH, U32))
+        def multiply_third_row(width):
             nc.vector.tensor_tensor(
-                room(upper, row + 2).rearrange("p (n j) -> p n j", j=RUN),
-                rooms[:, 1, :].rearrange("p (n j) -> p n j", j=RUN),
-                spread[1][:].rearrange("p j n -> p n j"),
+                rooms[:, 6, :width].rearrange("p (n j) -> p n j", j=RUN),
+                rooms[:, 1, :width].rearrange("p (n j) -> p n j", j=RUN),
+                spread_norm(1, 0, width),
                 MULT,
             )
-            width = (QUARTER, HALF)[g]
-            for start in range(0, HALF, width):
-                cols = slice(start, start + width)
-                gathered = looked_up(row + 3, HALF + start, width)
-                nc.vector.tensor_tensor(room(upper, row + 3)[:, cols], gathered, norm_sb[:, cols], MULT)
-            nc.scalar.activation(rooms[:, 2, :], looked_up(row + 3, 0, HALF), COPY)
-            if g == 0:
-                for start in (0, QUARTER):
-                    nc.gpsimd.tensor_scalar(*weave_upper(0, start), 1.0, 0.0, MULT, ADD)
-                weave_lower(1)
-                quantise(0, 0, 0, HALF)
-                quantise(0, 1, 0, HALF)
 
-        q_tiles = [
+        def gather_product(g, start):
+            cols = slice(start, start + QUARTER)
+            nc.vector.tensor_tensor(rooms[:, 5, cols], looked_up(g, 2, HALF + start, QUARTER), norm_upper[:, cols], MULT)
+
+        first_pair(0)
+        nc.scalar.activation(rooms[:, 1, :], looked_up(0, 3, HALF, HALF), COPY)
+        nc.scalar.activation(rooms[:, 0, :], looked_up(0, 3, 0, HALF), COPY)
+        multiply_third_row(HALF)
+        for start in (0, QUARTER):
+            gather_product(0, start)
+        nc.scalar.activation(rooms[:, 2, :], looked_up(0, 2, 0, HALF), COPY)
+        for start in (0, QUARTER):
+            nc.gpsimd.tensor_scalar(*weave(0, start, QUARTER), 1.0, 0.0, MULT, ADD)
+        multiply_lower(k_first[:, :HALF, 2:], rooms[:, 2::-2, :], 0, HALF)
+        for h in range(2):
+            cols = slice(h * HALF, (h + 1) * HALF)
+            quantise(first_codes[:, cols], first_scales[:, cols], k_first[:, cols, :])
+
+        first_pair(1)
+        seventh = flat[:, :N]
+        nc.scalar.activation(seventh[:, :SCALAR_SEVENTH], looked_up(1, 3, 0, SCALAR_SEVENTH), COPY)
+        nc.vector.tensor_copy(
+            seventh[:, SCALAR_SEVENTH:].bitcast(U32), looked_up(1, 3, SCALAR_SEVENTH, N - SCALAR_SEVENTH, U32)
+        )
+        nc.gpsimd.tensor_tensor(k_second[3][:, :, 3], rooms[:, 1, QUARTER:], norm_upper[:, QUARTER:], MULT)
+        multiply_third_row(QUARTER)
+
+        gather_product(1, 0)
+        nc.vector.tensor_copy(rooms[:, 5, QUARTER:].bitcast(U32), looked_up(1, 2, N - QUARTER, QUARTER, U32))
+        nc.scalar.activation(rooms[:, 2, :], looked_up(1, 2, 0, HALF), COPY)
+        nc.gpsimd.tensor_scalar(*weave(1, 0, GPSIMD_WEAVE), 1.0, 0.0, MULT, ADD)
+        nc.gpsimd.tensor_tensor(k_second[3][:, :, 2], rooms[:, 5, QUARTER:], norm_upper[:, QUARTER:], MULT)
+        nc.scalar.copy(*weave(1, GPSIMD_WEAVE, QUARTER - GPSIMD_WEAVE))
+        q_grouped = [
             keep.tile([P, NQ, PACK], BF16, name=f"q_grouped{g}", tag=tag, align_bytes=64)
             for g, tag in enumerate(("plane13", "plane12"))
         ]
-        q_grouped = [tile[:] for tile in q_tiles]
-        nc.gpsimd.tensor_scalar(*weave_upper(1, 0, 192), 1.0, 0.0, MULT, ADD)
         for g in range(PASSES):
             nc.scalar.copy(
-                q_grouped[g].rearrange("p (c i) t -> p c t i", i=4), q_raw[g][:].rearrange("p t (c i) -> p c t i", i=4)
+                q_grouped[g][:].rearrange("p (c i) t -> p c t i", i=4), q_raw[g][:].rearrange("p t (c i) -> p c t i", i=4)
             )
-        nc.scalar.copy(*weave_upper(1, 192, 64))
-        weave_lower(3, 0, 352)
-        quantise_q(0)
-        weave_lower(3, 352, 160)
-        merge(nc.scalar.copy, U32, 1)
-        nc.scalar.copy(*weave_upper(1, QUARTER))
-        merge(nc.vector.tensor_copy, I32, 0)
-        quantise_q(1)
-        quantise(1, 1, 0, QUARTER)
-        for i in (2, 0, 1, 3):
-            multiply(0, i)
-        multiply(1, 2)
-        for i in (0, 1):
-            quantise(1, 0, i * QUARTER, QUARTER)
-            multiply(1, i)
-        finish(2)
-        quantise(1, 1, QUARTER, QUARTER)
-        multiply(1, 3)
-        for i in (0, 1, 3):
+        multiply_lower(pairs[:, 1, :FIRST_CUT, :], rooms[:, 2::-2, :], 0, FIRST_CUT)
+        quantise(q_codes[0][:], q_scales[0][:], q_grouped[0][:])
+        multiply_lower(pairs[:, 1, FIRST_CUT:, :], rooms[:, 2::-2, :], FIRST_CUT, HALF - FIRST_CUT)
+        merge(nc.scalar.copy, U32, 0, QUARTER)
+        merge(nc.scalar.copy, U32, QUARTER, FIRST_CUT - QUARTER)
+        quantise_second(2)
+        quantise(q_codes[1][:], q_scales[1][:], q_grouped[1][:])
+        quantise_second(3)
+        merge(nc.vector.tensor_copy, I32, FIRST_CUT, HALF - FIRST_CUT)
+        quantise_second(0)
+        for g, i in ((0, 2), (0, 3), (0, 0), (0, 1), (1, 2), (1, 3), (1, 0)):
+            matmul(g, i)
+        quantise_second(1)
+        matmul(1, 1)
+        out_sb = keep.tile([P, N], F32, name="out_sb", tag="pairs", align_bytes=64)
+        for i in (2, 3, 0, 1):
             finish(i)

@@ -7,7 +7,6 @@ FLOPS = 2 * NQ * D * N
 F32 = mybir.dt.float32
 BF16 = mybir.dt.bfloat16
 U32 = mybir.dt.uint32
-I32 = mybir.dt.int32
 U16 = mybir.dt.uint16
 U8 = mybir.dt.uint8
 FP8X4 = mybir.dt.float8_e4m3fn_x4
@@ -24,9 +23,9 @@ QUARTER = N // 4
 RUN = HALF // P
 
 LOAD_ORDER = (0, 1, 3, 2)
-SCALAR_SEVENTH = 640
-GPSIMD_WEAVE = 160
-FIRST_CUT = 384
+VECTOR_SEVENTH = 448
+GPSIMD_WEAVE = (160, 128)
+FIRST_CUT = 256
 
 
 def tile_attend_pq_lin_bias_kernel(tc, qT, cb, norm, bias, offs, offs2, out):
@@ -51,17 +50,19 @@ def tile_attend_pq_lin_bias_kernel(tc, qT, cb, norm, bias, offs, offs2, out):
             keep.tile([P, PACK, NQ], F32, name="q_raw0", align_bytes=64),
             late.tile([P, PACK, NQ], F32, name="q_raw1", align_bytes=64, offset=1024),
         ]
-        q_codes = [keep.tile([P, NQ], U32, name=f"q_codes{g}", align_bytes=64) for g in range(PASSES)]
-        q_scales = [keep.tile([P, NQ], U8, name=f"q_scales{g}", align_bytes=64) for g in range(PASSES)]
         k_first = keep.tile([P, N, PACK], BF16, name="k_first", align_bytes=64)
         k_second = [
             late.tile([P, QUARTER, PACK], BF16, name=f"k_second{i}", align_bytes=64, offset=2048 * i) for i in range(2)
-        ] + [keep.tile([P, QUARTER, PACK], BF16, name=f"k_second{i}", align_bytes=64) for i in (2, 3)]
+        ]
+        k_upper = keep.tile([P, HALF + NQ, PACK], BF16, name="k_upper", align_bytes=64)
         pairs = keep.tile([P, 2, HALF, 2], BF16, name="pairs", align_bytes=64)
         first_codes = keep.tile([P, N], U32, name="first_codes", align_bytes=64)
         first_scales = keep.tile([P, N], U8, name="first_scales", align_bytes=64)
-        second_codes = [keep.tile([P, QUARTER], U32, name=f"second_codes{i}", align_bytes=64) for i in range(4)]
-        second_scales = [keep.tile([P, QUARTER], U8, name=f"second_scales{i}", align_bytes=64) for i in range(4)]
+        widths = (QUARTER, QUARTER, QUARTER, QUARTER + NQ)
+        second_codes = [keep.tile([P, w], U32, name=f"second_codes{i}", align_bytes=64) for i, w in enumerate(widths)]
+        second_scales = [keep.tile([P, w], U8, name=f"second_scales{i}", align_bytes=64) for i, w in enumerate(widths)]
+        q_codes = [keep.tile([P, NQ], U32, name="q_codes", align_bytes=64)[:], second_codes[3][:, QUARTER:]]
+        q_scales = [keep.tile([P, NQ], U8, name="q_scales", align_bytes=64)[:], second_scales[3][:, QUARTER:]]
         banks = [psum.tile([P, QUARTER], F32, name=f"bank{i}") for i in range(4)]
         spread = [psum.tile([P, RUN, P], F32, name=f"spread{h}") for h in range(2)]
 
@@ -104,8 +105,7 @@ def tile_attend_pq_lin_bias_kernel(tc, qT, cb, norm, bias, offs, offs2, out):
         def upper_place(g, start, width):
             if g == 0:
                 return k_first[:, HALF + start : HALF + start + width, :]
-            i, col = divmod(start, QUARTER)
-            return k_second[2 + i][:, col : col + width, :]
+            return k_upper[:, start : start + width, :]
 
         def weave(g, start, width):
             return upper_place(g, start, width)[:, :, 2:], rooms[:, 5:, start : start + width].rearrange("p t c -> p c t")
@@ -120,16 +120,17 @@ def tile_attend_pq_lin_bias_kernel(tc, qT, cb, norm, bias, offs, offs2, out):
             nc.vector.quantize_mx(out=codes.bitcast(FP8X4), scales=scales, in_=grouped.rearrange("p c t -> p (c t)"))
 
         def quantise_second(i):
-            quantise(second_codes[i][:], second_scales[i][:], k_second[i][:])
+            grouped = k_second[i][:] if i < 2 else upper_place(1, (i - 2) * QUARTER, widths[i])
+            quantise(second_codes[i][:], second_scales[i][:], grouped)
 
         def matmul(g, i):
             cols = slice(i * QUARTER, (i + 1) * QUARTER)
             nc.tensor.matmul_mx(
                 out=banks[i][:],
-                lhsT=q_codes[g][:].bitcast(FP8X4),
-                lhsT_scale=q_scales[g][:],
-                rhs=(second_codes[i][:] if g else first_codes[:, cols]).bitcast(FP8X4),
-                rhs_scale=second_scales[i][:] if g else first_scales[:, cols],
+                lhsT=q_codes[g].bitcast(FP8X4),
+                lhsT_scale=q_scales[g],
+                rhs=(second_codes[i][:, :QUARTER] if g else first_codes[:, cols]).bitcast(FP8X4),
+                rhs_scale=second_scales[i][:, :QUARTER] if g else first_scales[:, cols],
                 start=(g == 0),
                 stop=(g == PASSES - 1),
             )
@@ -163,16 +164,19 @@ def tile_attend_pq_lin_bias_kernel(tc, qT, cb, norm, bias, offs, offs2, out):
                 MULT,
             )
 
-        def gather_product(g, start):
-            cols = slice(start, start + QUARTER)
-            nc.vector.tensor_tensor(rooms[:, 5, cols], looked_up(g, 2, HALF + start, QUARTER), norm_upper[:, cols], MULT)
+        def gather_product(g, start, width):
+            cols = slice(start, start + width)
+            nc.vector.tensor_tensor(rooms[:, 5, cols], looked_up(g, 2, HALF + start, width), norm_upper[:, cols], MULT)
+
+        def round_q(copy, g, grouped):
+            copy(grouped.rearrange("p (c i) t -> p c t i", i=4), q_raw[g][:].rearrange("p t (c i) -> p c t i", i=4))
 
         first_pair(0)
         nc.scalar.activation(rooms[:, 1, :], looked_up(0, 3, HALF, HALF), COPY)
         nc.scalar.activation(rooms[:, 0, :], looked_up(0, 3, 0, HALF), COPY)
         multiply_third_row(HALF)
         for start in (0, QUARTER):
-            gather_product(0, start)
+            gather_product(0, start, QUARTER)
         nc.scalar.activation(rooms[:, 2, :], looked_up(0, 2, 0, HALF), COPY)
         for start in (0, QUARTER):
             nc.gpsimd.tensor_scalar(*weave(0, start, QUARTER), 1.0, 0.0, MULT, ADD)
@@ -182,42 +186,29 @@ def tile_attend_pq_lin_bias_kernel(tc, qT, cb, norm, bias, offs, offs2, out):
             quantise(first_codes[:, cols], first_scales[:, cols], k_first[:, cols, :])
 
         first_pair(1)
-        seventh = flat[:, :N]
-        nc.scalar.activation(seventh[:, :SCALAR_SEVENTH], looked_up(1, 3, 0, SCALAR_SEVENTH), COPY)
-        nc.vector.tensor_copy(
-            seventh[:, SCALAR_SEVENTH:].bitcast(U32), looked_up(1, 3, SCALAR_SEVENTH, N - SCALAR_SEVENTH, U32)
-        )
-        nc.gpsimd.tensor_tensor(k_second[3][:, :, 3], rooms[:, 1, QUARTER:], norm_upper[:, QUARTER:], MULT)
-        multiply_third_row(QUARTER)
+        nc.scalar.activation(flat[:, VECTOR_SEVENTH:N], looked_up(1, 3, VECTOR_SEVENTH, N - VECTOR_SEVENTH), COPY)
+        nc.vector.tensor_copy(flat[:, :VECTOR_SEVENTH].bitcast(U32), looked_up(1, 3, 0, VECTOR_SEVENTH, U32))
+        multiply_third_row(HALF)
 
-        gather_product(1, 0)
-        nc.vector.tensor_copy(rooms[:, 5, QUARTER:].bitcast(U32), looked_up(1, 2, N - QUARTER, QUARTER, U32))
+        for start in (QUARTER, 0):
+            gather_product(1, start, QUARTER)
+        q_first = keep.tile([P, NQ, PACK], BF16, name="q_first", tag="plane13", align_bytes=64)
+        round_q(nc.vector.tensor_copy, 0, q_first[:])
         nc.scalar.activation(rooms[:, 2, :], looked_up(1, 2, 0, HALF), COPY)
-        nc.gpsimd.tensor_scalar(*weave(1, 0, GPSIMD_WEAVE), 1.0, 0.0, MULT, ADD)
-        nc.gpsimd.tensor_tensor(k_second[3][:, :, 2], rooms[:, 5, QUARTER:], norm_upper[:, QUARTER:], MULT)
-        nc.scalar.copy(*weave(1, GPSIMD_WEAVE, QUARTER - GPSIMD_WEAVE))
-        q_grouped = [
-            keep.tile([P, NQ, PACK], BF16, name=f"q_grouped{g}", tag=tag, align_bytes=64)
-            for g, tag in enumerate(("plane13", "plane12"))
-        ]
-        for g in range(PASSES):
-            nc.scalar.copy(
-                q_grouped[g][:].rearrange("p (c i) t -> p c t i", i=4), q_raw[g][:].rearrange("p t (c i) -> p c t i", i=4)
-            )
+        nc.gpsimd.tensor_scalar(*weave(1, 0, GPSIMD_WEAVE[0]), 1.0, 0.0, MULT, ADD)
+        nc.gpsimd.tensor_scalar(*weave(1, *GPSIMD_WEAVE), 1.0, 0.0, MULT, ADD)
+        round_q(nc.scalar.copy, 1, k_upper[:, HALF:, :])
+        nc.scalar.copy(*weave(1, sum(GPSIMD_WEAVE), HALF - sum(GPSIMD_WEAVE)))
         multiply_lower(pairs[:, 1, :FIRST_CUT, :], rooms[:, 2::-2, :], 0, FIRST_CUT)
-        quantise(q_codes[0][:], q_scales[0][:], q_grouped[0][:])
-        multiply_lower(pairs[:, 1, FIRST_CUT:, :], rooms[:, 2::-2, :], FIRST_CUT, HALF - FIRST_CUT)
-        merge(nc.scalar.copy, U32, 0, QUARTER)
-        merge(nc.scalar.copy, U32, QUARTER, FIRST_CUT - QUARTER)
-        quantise_second(2)
-        quantise(q_codes[1][:], q_scales[1][:], q_grouped[1][:])
-        quantise_second(3)
-        merge(nc.vector.tensor_copy, I32, FIRST_CUT, HALF - FIRST_CUT)
-        quantise_second(0)
-        for g, i in ((0, 2), (0, 3), (0, 0), (0, 1), (1, 2), (1, 3), (1, 0)):
-            matmul(g, i)
-        quantise_second(1)
-        matmul(1, 1)
-        out_sb = keep.tile([P, N], F32, name="out_sb", tag="pairs", align_bytes=64)
+        quantise(q_codes[0], q_scales[0], q_first[:])
         for i in (2, 3, 0, 1):
+            matmul(0, i)
+        multiply_lower(pairs[:, 1, FIRST_CUT:, :], rooms[:, 2::-2, :], FIRST_CUT, HALF - FIRST_CUT)
+        for start in (0, QUARTER):
+            merge(nc.scalar.copy, U32, start, QUARTER)
+        for i in (3, 2, 0, 1):
+            quantise_second(i)
+            matmul(1, i)
+        out_sb = keep.tile([P, N], F32, name="out_sb", tag="pairs", align_bytes=64)
+        for i in (3, 2, 0, 1):
             finish(i)

@@ -24,8 +24,8 @@ RUN = HALF // P
 
 LOAD_ORDER = (0, 1, 3, 2)
 VECTOR_SEVENTH = 448
-GPSIMD_WEAVE = (160, 128)
-FIRST_CUT = 256
+GPSIMD_WEAVE = (48, 208)
+FIRST_CUT = 128
 
 
 def tile_attend_pq_lin_bias_kernel(tc, qT, cb, norm, bias, offs, offs2, out):
@@ -203,7 +203,8 @@ def tile_attend_pq_lin_bias_kernel(tc, qT, cb, norm, bias, offs, offs2, out):
         quantise(q_codes[0], q_scales[0], q_first[:])
         for i in (2, 3, 0, 1):
             matmul(0, i)
-        multiply_lower(pairs[:, 1, FIRST_CUT:, :], rooms[:, 2::-2, :], FIRST_CUT, HALF - FIRST_CUT)
+        for start, stop in ((FIRST_CUT, QUARTER), (QUARTER, HALF)):
+            multiply_lower(pairs[:, 1, start:stop, :], rooms[:, 2::-2, :], start, stop - start)
         for start in (0, QUARTER):
             merge(nc.scalar.copy, U32, start, QUARTER)
         for i in (3, 2, 0, 1):

@@ -25,6 +25,8 @@ RUN = HALF // P
 LOAD_ORDER = (0, 1, 3, 2)
 VECTOR_SEVENTH = 448
 GPSIMD_WEAVE = (48, 208)
+SCALAR_WEAVE = 128
+GPSIMD_SEVENTH = 192
 FIRST_CUT = 128
 
 
@@ -178,8 +180,9 @@ def tile_attend_pq_lin_bias_kernel(tc, qT, cb, norm, bias, offs, offs2, out):
         for start in (0, QUARTER):
             gather_product(0, start, QUARTER)
         nc.scalar.activation(rooms[:, 2, :], looked_up(0, 2, 0, HALF), COPY)
-        for start in (0, QUARTER):
-            nc.gpsimd.tensor_scalar(*weave(0, start, QUARTER), 1.0, 0.0, MULT, ADD)
+        for start, stop in ((0, QUARTER), (QUARTER, HALF - SCALAR_WEAVE)):
+            nc.gpsimd.tensor_scalar(*weave(0, start, stop - start), 1.0, 0.0, MULT, ADD)
+        nc.scalar.copy(*weave(0, HALF - SCALAR_WEAVE, SCALAR_WEAVE))
         multiply_lower(k_first[:, :HALF, 2:], rooms[:, 2::-2, :], 0, HALF)
         for h in range(2):
             cols = slice(h * HALF, (h + 1) * HALF)
@@ -188,7 +191,9 @@ def tile_attend_pq_lin_bias_kernel(tc, qT, cb, norm, bias, offs, offs2, out):
         first_pair(1)
         nc.scalar.activation(flat[:, VECTOR_SEVENTH:N], looked_up(1, 3, VECTOR_SEVENTH, N - VECTOR_SEVENTH), COPY)
         nc.vector.tensor_copy(flat[:, :VECTOR_SEVENTH].bitcast(U32), looked_up(1, 3, 0, VECTOR_SEVENTH, U32))
-        multiply_third_row(HALF)
+        multiply_third_row(HALF - GPSIMD_SEVENTH)
+        cols = slice(HALF - GPSIMD_SEVENTH, HALF)
+        nc.gpsimd.tensor_tensor(rooms[:, 6, cols], rooms[:, 1, cols], norm_upper[:, cols], MULT)
 
         for start in (QUARTER, 0):
             gather_product(1, start, QUARTER)

import concourse.mybir as mybir
from concourse.masks import make_identity

NQ, D, N, C = 128, 1024, 1024, 2048
FLOPS = 2 * NQ * D * N

F32 = mybir.dt.float32
BF16 = mybir.dt.bfloat16
U32 = mybir.dt.uint32
U16 = mybir.dt.uint16
U8 = mybir.dt.uint8
FP8X4 = mybir.dt.float8_e4m3fn_x4
MULT = mybir.AluOpType.mult
ADD = mybir.AluOpType.add
COPY = mybir.ActivationFunctionType.Copy

P = 128
PACK = 4
PASSES = D // (P * PACK)
LIST = 16
HALF = N // 2
QUARTER = N // 4
RUN = HALF // P

LOAD_ORDER = (0, 1, 3, 2)
VECTOR_SEVENTH = 448
GPSIMD_WEAVE = (48, 208)
SCALAR_WEAVE = 128
GPSIMD_SEVENTH = 192
FIRST_CUT = 128


def tile_attend_pq_lin_bias_kernel(tc, qT, cb, norm, bias, offs, offs2, out):
    nc = tc.nc
    cb_planes = cb.rearrange("(g p t) c -> g t p c", g=PASSES, t=PACK)
    q_rows = qT[0].rearrange("(g p t) q -> g p t q", g=PASSES, t=PACK)

    with (
        tc.tile_pool(name="keep", bufs=1) as keep,
        tc.tile_pool(name="late", bufs=1) as late,
        tc.psum_pool(name="psum", bufs=1) as psum,
    ):
        lists = [keep.tile([P, N // LIST], U16, name=f"list{g}") for g in range(PASSES)]
        norm_runs = keep.tile([P, 2, 2 * RUN], F32, name="norm_runs")
        identity = keep.tile([P, P], F32, name="identity")
        norm_upper = keep.tile([P, HALF], F32, name="norm_upper")
        bias_sb = keep.tile([P, N], F32, name="bias_sb")
        planes = [
            [keep.tile([P, C], F32, name=f"plane{g}{t}", align_bytes=64) for t in range(PACK)] for g in range(PASSES)
        ]
        q_raw = [
            keep.tile([P, PACK, NQ], F32, name="q_raw0", align_bytes=64),
            late.tile([P, PACK, NQ], F32, name="q_raw1", align_bytes=64, offset=1024),
        ]
        k_first = keep.tile([P, N, PACK], BF16, name="k_first", align_bytes=64)
        k_second = [
            late.tile([P, QUARTER, PACK], BF16, name=f"k_second{i}", align_bytes=64, offset=2048 * i) for i in range(2)
        ]
        k_upper = keep.tile([P, HALF + NQ, PACK], BF16, name="k_upper", align_bytes=64)
        pairs = keep.tile([P, 2, HALF, 2], BF16, name="pairs", align_bytes=64)
        first_codes = keep.tile([P, N], U32, name="first_codes", align_bytes=64)
        first_scales = keep.tile([P, N], U8, name="first_scales", align_bytes=64)
        widths = (QUARTER, QUARTER, QUARTER, QUARTER + NQ)
        second_codes = [keep.tile([P, w], U32, name=f"second_codes{i}", align_bytes=64) for i, w in enumerate(widths)]
        second_scales = [keep.tile([P, w], U8, name=f"second_scales{i}", align_bytes=64) for i, w in enumerate(widths)]
        q_codes = [keep.tile([P, NQ], U32, name="q_codes", align_bytes=64)[:], second_codes[3][:, QUARTER:]]
        q_scales = [keep.tile([P, NQ], U8, name="q_scales", align_bytes=64)[:], second_scales[3][:, QUARTER:]]
        banks = [psum.tile([P, QUARTER], F32, name=f"bank{i}") for i in range(4)]
        spread = [psum.tile([P, RUN, P], F32, name=f"spread{h}") for h in range(2)]

        nc.sync.dma_start(norm_runs[:, :, :RUN], norm[0].rearrange("(h p j) -> p h j", h=2, j=RUN))
        for g in range(PASSES):
            for place, t in enumerate(LOAD_ORDER):
                if (g, place) == (1, 0):
                    nc.sync.dma_start(lists[1][:], offs2)
                nc.sync.dma_start(planes[g][t][:], cb_planes[g, t])
                if (g, place) == (0, 0):
                    nc.sync.dma_start(lists[0][:], offs)
        for g in range(PASSES):
            nc.sync.dma_start(q_raw[g][:], q_rows[g])
        nc.sync.dma_start(bias_sb[:], bias)

        make_identity(nc, identity[:])
        for h in (1, 0):
            for j in range(RUN):
                column = norm_runs[:, h, j : j + 1]
                nc.tensor.transpose(spread[h][:, j, :], column.to_broadcast([P, P]), identity[:])
        nc.scalar.copy(norm_upper[:].rearrange("p (n j) -> p n j", j=RUN), spread[1][:].rearrange("p j n -> p n j"))

        rooms = keep.tile([P, 7, HALF], F32, name="rooms", tag="norm_runs")
        flat = rooms[:].rearrange("p s c -> p (s c)")

        def looked_up(g, t, start, width, dtype=F32):
            return planes[g][t][:].bitcast(dtype).indirect(lists[g][:, start // LIST : (start + width) // LIST])

        def spread_norm(h, start, width):
            return spread[h][:, :, start // RUN : (start + width) // RUN].rearrange("p j n -> p n j")

        def multiply_lower(woven, rows, start, width):
            nc.vector.tensor_tensor(
                woven.rearrange("p (n j) t -> p n j t", j=RUN),
                rows[:, :, start : start + width].rearrange("p t (n j) -> p n j t", j=RUN),
                spread_norm(0, start, width).unsqueeze(3).to_broadcast([P, width // RUN, RUN, 2]),
                MULT,
            )

        def upper_place(g, start, width):
            if g == 0:
                return k_first[:, HALF + start : HALF + start + width, :]
            return k_upper[:, start : start + width, :]

        def weave(g, start, width):
            return upper_place(g, start, width)[:, :, 2:], rooms[:, 5:, start : start + width].rearrange("p t c -> p c t")

        def merge(copy, dtype, start, width):
            words = pairs[:].rearrange("p u c t -> p u (c t)").bitcast(dtype)[:, :, start : start + width]
            i, col = divmod(start, QUARTER)
            merged = k_second[i][:, col : col + width, :].rearrange("p c t -> p (c t)").bitcast(dtype)
            copy(merged.rearrange("p (c u) -> p c u", u=2), words.rearrange("p u c -> p c u"))

        def quantise(codes, scales, grouped):
            nc.vector.quantize_mx(out=codes.bitcast(FP8X4), scales=scales, in_=grouped.rearrange("p c t -> p (c t)"))

        def quantise_second(i):
            grouped = k_second[i][:] if i < 2 else upper_place(1, (i - 2) * QUARTER, widths[i])
            quantise(second_codes[i][:], second_scales[i][:], grouped)

        def matmul(g, i):
            cols = slice(i * QUARTER, (i + 1) * QUARTER)
            nc.tensor.matmul_mx(
                out=banks[i][:],
                lhsT=q_codes[g].bitcast(FP8X4),
                lhsT_scale=q_scales[g],
                rhs=(second_codes[i][:, :QUARTER] if g else first_codes[:, cols]).bitcast(FP8X4),
                rhs_scale=second_scales[i][:, :QUARTER] if g else first_scales[:, cols],
                start=(g == 0),
                stop=(g == PASSES - 1),
            )

        def finish(i):
            cols = slice(i * QUARTER, (i + 1) * QUARTER)
            nc.vector.tensor_tensor(out_sb[:, cols], banks[i][:], bias_sb[:, cols], ADD)
            nc.sync.dma_start(out[0][:, cols], out_sb[:, cols])

        def first_pair(g):
            nc.scalar.activation(flat[:, 3 * HALF : 5 * HALF], looked_up(g, 0, 0, N), COPY)
            for start in (0, QUARTER):
                words = rooms[:, 5, start : start + QUARTER].bitcast(U32)
                nc.vector.tensor_copy(words, looked_up(g, 1, HALF + start, QUARTER, U32))
            nc.scalar.activation(rooms[:, 2, :], looked_up(g, 1, 0, HALF), COPY)
            for start in (0, QUARTER):
                cols = slice(start, start + QUARTER)
                nc.gpsimd.tensor_tensor(
                    upper_place(g, start, QUARTER)[:, :, :2],
                    rooms[:, 4:6, cols].rearrange("p t c -> p c t"),
                    norm_upper[:, cols].unsqueeze(2).to_broadcast([P, QUARTER, 2]),
                    MULT,
                )
            multiply_lower(pairs[:, 0, :, :] if g else k_first[:, :HALF, :2], rooms[:, 3:1:-1, :], 0, HALF)

        def multiply_third_row(width):
            nc.vector.tensor_tensor(
                rooms[:, 6, :width].rearrange("p (n j) -> p n j", j=RUN),
                rooms[:, 1, :width].rearrange("p (n j) -> p n j", j=RUN),
                spread_norm(1, 0, width),
                MULT,
            )

        def gather_product(g, start, width):
            cols = slice(start, start + width)
            nc.vector.tensor_tensor(rooms[:, 5, cols], looked_up(g, 2, HALF + start, width), norm_upper[:, cols], MULT)

        def round_q(copy, g, grouped):
            copy(grouped.rearrange("p (c i) t -> p c t i", i=4), q_raw[g][:].rearrange("p t (c i) -> p c t i", i=4))

        first_pair(0)
        nc.scalar.activation(rooms[:, 1, :], looked_up(0, 3, HALF, HALF), COPY)
        nc.scalar.activation(rooms[:, 0, :], looked_up(0, 3, 0, HALF), COPY)
        multiply_third_row(HALF)
        for start in (0, QUARTER):
            gather_product(0, start, QUARTER)
        nc.scalar.activation(rooms[:, 2, :], looked_up(0, 2, 0, HALF), COPY)
        for start, stop in ((0, QUARTER), (QUARTER, HALF - SCALAR_WEAVE)):
            nc.gpsimd.tensor_scalar(*weave(0, start, stop - start), 1.0, 0.0, MULT, ADD)
        nc.scalar.copy(*weave(0, HALF - SCALAR_WEAVE, SCALAR_WEAVE))
        multiply_lower(k_first[:, :HALF, 2:], rooms[:, 2::-2, :], 0, HALF)
        for h in range(2):
            cols = slice(h * HALF, (h + 1) * HALF)
            quantise(first_codes[:, cols], first_scales[:, cols], k_first[:, cols, :])

        first_pair(1)
        nc.scalar.activation(flat[:, VECTOR_SEVENTH:N], looked_up(1, 3, VECTOR_SEVENTH, N - VECTOR_SEVENTH), COPY)
        nc.vector.tensor_copy(flat[:, :VECTOR_SEVENTH].bitcast(U32), looked_up(1, 3, 0, VECTOR_SEVENTH, U32))
        multiply_third_row(HALF - GPSIMD_SEVENTH)
        cols = slice(HALF - GPSIMD_SEVENTH, HALF)
        nc.gpsimd.tensor_tensor(rooms[:, 6, cols], rooms[:, 1, cols], norm_upper[:, cols], MULT)

        for start in (QUARTER, 0):
            gather_product(1, start, QUARTER)
        q_first = keep.tile([P, NQ, PACK], BF16, name="q_first", tag="plane13", align_bytes=64)
        round_q(nc.vector.tensor_copy, 0, q_first[:])
        nc.scalar.activation(rooms[:, 2, :], looked_up(1, 2, 0, HALF), COPY)
        nc.gpsimd.tensor_scalar(*weave(1, 0, GPSIMD_WEAVE[0]), 1.0, 0.0, MULT, ADD)
        nc.gpsimd.tensor_scalar(*weave(1, *GPSIMD_WEAVE), 1.0, 0.0, MULT, ADD)
        round_q(nc.scalar.copy, 1, k_upper[:, HALF:, :])
        nc.scalar.copy(*weave(1, sum(GPSIMD_WEAVE), HALF - sum(GPSIMD_WEAVE)))
        multiply_lower(pairs[:, 1, :FIRST_CUT, :], rooms[:, 2::-2, :], 0, FIRST_CUT)
        quantise(q_codes[0], q_scales[0], q_first[:])
        for i in (2, 3, 0, 1):
            matmul(0, i)
        for start, stop in ((FIRST_CUT, QUARTER), (QUARTER, HALF)):
            multiply_lower(pairs[:, 1, start:stop, :], rooms[:, 2::-2, :], start, stop - start)
        for start in (0, QUARTER):
            merge(nc.scalar.copy, U32, start, QUARTER)
        for i in (3, 2, 0, 1):
            quantise_second(i)
            matmul(1, i)
        out_sb = keep.tile([P, N], F32, name="out_sb", tag="pairs", align_bytes=64)
        for i in (3, 2, 0, 1):
            finish(i)
